import numpy as np
import ml_dtypes


def mxq(x, axis, fmt="e4m3"):
    dtype, down = {"e4m3": (ml_dtypes.float8_e4m3fn, 7), "e5m2": (ml_dtypes.float8_e5m2, 14)}[fmt]
    v = np.moveaxis(np.asarray(x, np.float32).astype(ml_dtypes.bfloat16).astype(np.float64), axis, -1)
    blocks = v.reshape(v.shape[:-1] + (-1, 32))
    amax = np.abs(blocks).max(-1, keepdims=True)
    byte = np.maximum(np.where(amax > 0, np.frexp(amax)[1] - 1 + 127, 0) - down, 1)
    scale = np.exp2(byte - 127.0)
    codes = (blocks / scale).astype(np.float32).astype(dtype).astype(np.float64)
    return np.moveaxis((codes * scale).reshape(v.shape), -1, axis)


WIDE = False


def mx_kscale(k):
    if not WIDE:
        return np.ones(k)
    levels = np.array([10, -10, 5, -5, 0])
    if k % 512:
        return np.exp2(np.random.permutation(np.resize(levels, k // 32))).repeat(32)
    a = np.empty((k // 512, 16))
    for p in range(k // 512):
        a[p, :8] = np.random.permutation(np.resize(levels, 8))
        for g in range(8):
            far = levels[np.abs(levels - a[p, g]) >= 10]
            a[p, g + 8] = far[np.random.randint(len(far))]
    return np.exp2(a.ravel()).repeat(32)


def f64(x):
    return np.asarray(x).astype(np.float64)


def striped(idx):
    return np.tile(np.asarray(idx).reshape(-1, 16).T, (8, 1)).astype(np.uint16)


def unstriped(offs):
    return offs[:16].T.reshape(-1).astype(np.int64)


E2M1 = np.array([0.0, 0.5, 1.0, 1.5, 2.0, 3.0, 4.0, 6.0, -0.0, -0.5, -1.0, -1.5, -2.0, -3.0, -4.0, -6.0])


def pack_weight(w, fmt):
    k, n = w.shape
    w = f64(np.asarray(w, np.float32).astype(ml_dtypes.bfloat16)).reshape(k // 32, 32, n)
    amax = np.abs(w).max(1)
    if fmt == "e4m3":
        byte = np.frexp(amax)[1] - 1 + 127 - 7
    else:
        mant, ex = np.frexp(amax / 6.0)
        byte = np.where(mant > 0.5, ex, ex - 1) + 127
    byte = np.clip(np.where(amax > 0, byte, 1), 1, 254)
    scaled = (w * np.exp2(127.0 - byte)[:, None, :]).reshape(k, n).astype(np.float32)
    by_word = np.ascontiguousarray(scaled.reshape(k // 512, 128, 4, n).transpose(0, 1, 3, 2))
    if fmt == "e4m3":
        words = by_word.astype(ml_dtypes.float8_e4m3fn).view(np.uint8)
    else:
        c = by_word.astype(ml_dtypes.float4_e2m1fn).view(np.uint8) & 0xF
        words = (c[..., 0::2] | (c[..., 1::2] << 4)).reshape(k // 512, 128, 2 * n)
    return np.ascontiguousarray(words), np.ascontiguousarray(byte.astype(np.uint8).reshape(k // 512, 16, n))


def unpack_weight(words, scales, fmt):
    g, _, n = scales.shape
    words = np.ascontiguousarray(words).reshape(g, 128, n, -1)
    if fmt == "e4m3":
        vals = words.view(ml_dtypes.float8_e4m3fn).astype(np.float64)
    else:
        nib = np.empty((g, 128, n, 4), np.uint8)
        nib[..., 0::2] = words & 0xF
        nib[..., 1::2] = words >> 4
        vals = E2M1[nib]
    vals = vals * np.repeat(np.exp2(scales.astype(np.float64) - 127.0), 8, axis=1)[..., None]
    return vals.transpose(0, 1, 3, 2).reshape(g * 512, n)


B, N, T, D, NQ = 1, 512, 2048, 1024, 256


def setup_inputs():
    n = np.random.standard_normal
    idx = np.random.permutation(T)[:B * N]
    s = mx_kscale(D)[:, None]
    kp = pack_weight(n((D, T)) / s, "e2m1")
    return {
        "qT": (n((B, D, NQ)) * s * (1.00 / np.sqrt(D))).astype(np.float32),
        "k_words": np.ascontiguousarray(kp[0].reshape(1, 2, 128, T, 2).transpose(0, 2, 3, 1, 4)).reshape(1, 128, T, 4),
        "k_scales": kp[1],
        "kn": np.tile(np.random.uniform(1.0, 4.0, 2048), (128, 1)).astype(np.float32),
        "qn": (np.random.uniform(1.0, 4.0, (B, NQ, 1))).astype(np.float32),
        "offs": striped(idx),
    }


def reference(qT, k_words, k_scales, kn, qn, offs):
    idx = unstriped(offs)
    pick = lambda x, which: x[:, which].reshape(x.shape[0], B, -1).transpose(1, 0, 2)
    k = unpack_weight(k_words.reshape(1, 128, T, 2, 2).transpose(0, 3, 1, 2, 4).reshape(2, 128, 2 * T), k_scales, "e2m1")
    kg = pick(k, idx)
    qq = mxq(f64(qT), 1, "e4m3")
    a = qq.transpose(0, 2, 1) @ kg
    y = np.maximum(f64(qn) + pick(f64(kn), idx)[:, :1, :] - 2.0 * a, 0.0)
    return y

@@ -1,0 +1,138 @@
+from contextlib import ExitStack
+
+import concourse.mybir as mybir
+from concourse.masks import make_identity
+
+N, T, D, NQ = 512, 2048, 1024, 256
+FLOPS = 2 * NQ * N * D
+BYTES = 4 * D * NQ + 128 * T * 4 + 32 * T + 4 * T + 4 * NQ + 128 * 32 * 2 + 4 * NQ * N
+
+F32 = mybir.dt.float32
+BF16 = mybir.dt.bfloat16
+I32 = mybir.dt.int32
+U32 = mybir.dt.uint32
+U16 = mybir.dt.uint16
+U8 = mybir.dt.uint8
+FP8X4 = mybir.dt.float8_e4m3fn_x4
+FP4X4 = mybir.dt.float4_e2m1fn_x4
+ALU = mybir.AluOpType
+ACT = mybir.ActivationFunctionType
+
+P = 128
+PASSES = 2
+QT = 2
+HALF = N // 2
+
+
+def tile_attend_infodist_topk_kernel(tc, qT, k_words, k_scales, kn, qn, offs, out):
+    nc = tc.nc
+    with ExitStack() as ctx:
+        sb = ctx.enter_context(tc.tile_pool(name="sb", bufs=1))
+        ps = ctx.enter_context(tc.psum_pool(name="ps", bufs=1))
+
+        scale_win = sb.tile([P, T // 4], I32, name="scale_win", align_bytes=64)
+        nc.sync.dma_start(scale_win[96:128, :], k_scales.bitcast(I32).rearrange("o f w -> f o w"))
+        offsets = sb.tile([P, N // 16], U16, name="offsets")
+        nc.sync.dma_start(offsets[:], offs)
+        nc.vector.memset(scale_win[0:96, :], 0)
+
+        kn_win = sb.tile([P, T], F32, name="kn_win", align_bytes=64)
+        nc.sync.dma_start(kn_win[127:128, :], kn[0:1, :])
+
+        word_win = sb.tile([P, T], I32, name="word_win", align_bytes=64)
+        nc.scalar.dma_start(word_win[:], k_words[0].rearrange("p t b -> p (t b)").bitcast(I32))
+
+        q_raw = []
+        for o in range(PASSES):
+            raw = sb.tile([P, 4, NQ], F32, name="q_raw%d" % o, align_bytes=64)
+            nc.scalar.dma_start(raw[:], qT[0, 512 * o : 512 * (o + 1), :].rearrange("(p t) q -> p t q", t=4))
+            q_raw.append(raw)
+
+        qn_col = sb.tile([P, QT], F32, name="qn_col")
+        with nc.allow_non_contiguous_dma(reason="one number a partition and query tile"):
+            nc.sync.dma_start(qn_col[:], qn[0].rearrange("(j p) o -> p (j o)", p=P))
+
+        k_planes = sb.tile([P, PASSES * N // 4], I32, name="k_planes", align_bytes=64)
+        nc.vector.memset(kn_win[0:127, :], 0.0)
+        nc.vector.memset(k_planes[:], 0)
+
+        ident = sb.tile([P, P], F32, name="ident")
+        make_identity(nc, ident[:])
+
+        scale_g = sb.tile([P, N], U8, name="scale_g", align_bytes=64)
+        nc.vector.tensor_copy(scale_g[:], scale_win[:].bitcast(U8).indirect(offsets[:]))
+        for quad in range(4):
+            nc.sync.dma_start(
+                k_planes[32 * quad : 32 * quad + 4, :],
+                scale_g[:].bitcast(I32)[96 + 8 * quad : 96 + 8 * quad + 8, :],
+            )
+
+        kn_g = sb.tile([P, N], F32, name="kn_g", align_bytes=64)
+        nc.vector.tensor_copy(kn_g[:], kn_win[:].indirect(offsets[:]))
+        kn_turned = ps.tile([P, 4, P], F32, name="kn_turned")
+        for b in range(4):
+            nc.tensor.transpose(kn_turned[:, b, :], kn_g[:, P * b : P * (b + 1)], ident[:])
+        kn_col = sb.tile([P, 4], F32, name="kn_col")
+        nc.scalar.copy(kn_col[:], kn_turned[:, :, P - 1])
+        kn_spread = ps.tile([P, N], F32, name="kn_spread")
+        for b in range(4):
+            nc.tensor.transpose(kn_spread[:, P * b : P * (b + 1)], kn_col[:, b : b + 1].to_broadcast([P, P]), ident[:])
+
+        word_g = sb.tile([P, N], U32, name="word_g", align_bytes=64)
+        nc.vector.tensor_copy(word_g[:], word_win[:].bitcast(U32).indirect(offsets[:]))
+        k_codes = []
+        for o in range(PASSES):
+            codes = sb.tile([P, 2 * N], U8, name="k_codes%d" % o, align_bytes=64)
+            nc.vector.tensor_copy(codes[:].bitcast(U16), word_g[:].bitcast(U16)[:, o : 2 * N : 2])
+            k_codes.append(codes)
+
+        q_codes, q_planes = {}, {}
+        for o, j in ((0, 0), (0, 1), (1, 0), (1, 1)):
+            grouped = sb.tile([P, P, 4], BF16, name="grouped%d%d" % (o, j), align_bytes=64)
+            src = q_raw[o][:, :, P * j : P * (j + 1)].rearrange("p t m -> p m t")
+            if (o, j) == (1, 0):
+                nc.vector.tensor_copy(grouped[:], src)
+            else:
+                nc.scalar.copy(grouped[:], src)
+            codes = sb.tile([P, P], U32, name="q_codes%d%d" % (o, j), align_bytes=64)
+            plane = sb.tile([P, P], U8, name="q_plane%d%d" % (o, j), align_bytes=64)
+            nc.vector.quantize_mx(
+                out=codes[:].bitcast(FP8X4), scales=plane[:], in_=grouped[:].rearrange("p m t -> p (m t)")
+            )
+            q_codes[(o, j)], q_planes[(o, j)] = codes, plane
+
+        kn_rows = sb.tile([P, N], F32, name="kn_rows", align_bytes=64)
+        nc.scalar.copy(kn_rows[:], kn_spread[:])
+
+        def product(acc, o, j, c0, c1):
+            nc.tensor.matmul_mx(
+                out=acc,
+                lhsT=q_codes[(o, j)][:].bitcast(FP8X4),
+                lhsT_scale=q_planes[(o, j)][:],
+                rhs=k_codes[o][:, 2 * c0 : 2 * c1].bitcast(FP4X4),
+                rhs_scale=k_planes[:].bitcast(U8)[:, N * o + c0 : N * o + c1],
+                start=(o == 0),
+                stop=(o == PASSES - 1),
+            )
+
+        def finish(acc, res, j, c0, c1):
+            part = sb.tile([P, c1 - c0], F32, name="part%d_%d" % (j, c0))
+            nc.vector.scalar_tensor_tensor(part[:], acc, -2.0, kn_rows[:, c0:c1], ALU.mult, ALU.add)
+            nc.scalar.activation(res, part[:], ACT.Relu, bias=qn_col[:, j : j + 1])
+
+        acc0 = ps.tile([P, N], F32, name="acc0")
+        acc1 = [ps.tile([P, P], F32, name="acc1_%d" % b) for b in range(4)]
+        for o in range(PASSES):
+            product(acc0[:], o, 0, 0, N)
+        for o in range(PASSES):
+            for b in range(4):
+                product(acc1[b][:], o, 1, P * b, P * (b + 1))
+        for h in range(2):
+            res = sb.tile([P, HALF], F32, name="res0_%d" % h)
+            finish(acc0[:, HALF * h : HALF * (h + 1)], res[:], 0, HALF * h, HALF * (h + 1))
+            nc.sync.dma_start(out[0, 0:P, HALF * h : HALF * (h + 1)], res[:])
+        for h in range(2):
+            res = sb.tile([P, HALF], F32, name="res1_%d" % h)
+            for b in (2 * h, 2 * h + 1):
+                finish(acc1[b][:], res[:, P * (b % 2) : P * (b % 2 + 1)], 1, P * b, P * (b + 1))
+            nc.sync.dma_start(out[0, P : 2 * P, HALF * h : HALF * (h + 1)], res[:])

@@ -30,6 +30,11 @@ def tile_attend_infodist_topk_kernel(tc, qT, k_words, k_scales, kn, qn, offs, ou
         sb = ctx.enter_context(tc.tile_pool(name="sb", bufs=1))
         ps = ctx.enter_context(tc.psum_pool(name="ps", bufs=1))
 
+        zero_col = sb.tile([P, 1], F32, name="zero_col")
+        nc.vector.memset(zero_col[:], 0.0)
+        qn_rows = sb.tile([P, P], F32, name="qn_rows")
+        nc.scalar.copy(qn_rows[0 : P - QT, :], zero_col[0 : P - QT, :].to_broadcast([P - QT, P]))
+
         scale_win = sb.tile([P, T // 4], I32, name="scale_win", align_bytes=64)
         nc.sync.dma_start(scale_win[96:128, :], k_scales.bitcast(I32).rearrange("o f w -> f o w"))
         offsets = sb.tile([P, N // 16], U16, name="offsets")
@@ -40,17 +45,15 @@ def tile_attend_infodist_topk_kernel(tc, qT, k_words, k_scales, kn, qn, offs, ou
         nc.sync.dma_start(kn_win[127:128, :], kn[0:1, :])
 
         word_win = sb.tile([P, T], I32, name="word_win", align_bytes=64)
-        nc.scalar.dma_start(word_win[:], k_words[0].rearrange("p t b -> p (t b)").bitcast(I32))
+        nc.sync.dma_start(word_win[:], k_words[0].rearrange("p t b -> p (t b)").bitcast(I32))
 
         q_raw = []
         for o in range(PASSES):
             raw = sb.tile([P, 4, NQ], F32, name="q_raw%d" % o, align_bytes=64)
-            nc.scalar.dma_start(raw[:], qT[0, 512 * o : 512 * (o + 1), :].rearrange("(p t) q -> p t q", t=4))
+            nc.sync.dma_start(raw[:], qT[0, 512 * o : 512 * (o + 1), :].rearrange("(p t) q -> p t q", t=4))
             q_raw.append(raw)
 
-        qn_col = sb.tile([P, QT], F32, name="qn_col")
-        with nc.allow_non_contiguous_dma(reason="one number a partition and query tile"):
-            nc.sync.dma_start(qn_col[:], qn[0].rearrange("(j p) o -> p (j o)", p=P))
+        nc.scalar.dma_start(qn_rows[P - QT : P, :], qn[0].rearrange("(j p) o -> j (p o)", p=P))
 
         k_planes = sb.tile([P, PASSES * N // 4], I32, name="k_planes", align_bytes=64)
         nc.vector.memset(kn_win[0:127, :], 0.0)
@@ -58,11 +61,15 @@ def tile_attend_infodist_topk_kernel(tc, qT, k_words, k_scales, kn, qn, offs, ou
 
         ident = sb.tile([P, P], F32, name="ident")
         make_identity(nc, ident[:])
+        qn_turned = ps.tile([P, P], F32, name="qn_turned")
+        nc.tensor.transpose(qn_turned[:], qn_rows[:], ident[:])
+        qn_col = sb.tile([P, QT], F32, name="qn_col")
+        nc.scalar.copy(qn_col[:], qn_turned[:, P - QT : P])
 
         scale_g = sb.tile([P, N], U8, name="scale_g", align_bytes=64)
         nc.vector.tensor_copy(scale_g[:], scale_win[:].bitcast(U8).indirect(offsets[:]))
         for quad in range(4):
-            nc.sync.dma_start(
+            nc.scalar.dma_start(
                 k_planes[32 * quad : 32 * quad + 4, :],
                 scale_g[:].bitcast(I32)[96 + 8 * quad : 96 + 8 * quad + 8, :],
             )

@@ -125,7 +125,10 @@ def tile_attend_infodist_topk_kernel(tc, qT, k_words, k_scales, kn, qn, offs, ou
         def finish(acc, res, j, c0, c1):
             part = sb.tile([P, c1 - c0], F32, name="part%d_%d" % (j, c0))
             nc.vector.scalar_tensor_tensor(part[:], acc, -2.0, kn_rows[:, c0:c1], ALU.mult, ALU.add)
-            nc.scalar.activation(res, part[:], ACT.Relu, bias=qn_col[:, j : j + 1])
+            if j == 1 and c0 >= HALF:
+                nc.vector.tensor_scalar(res, part[:], qn_col[:, j : j + 1], 0.0, ALU.add, ALU.max)
+            else:
+                nc.scalar.activation(res, part[:], ACT.Relu, bias=qn_col[:, j : j + 1])
 
         acc0 = ps.tile([P, N], F32, name="acc0")
         acc1 = [ps.tile([P, P], F32, name="acc1_%d" % b) for b in range(4)]

@@ -49,7 +49,7 @@ def tile_attend_infodist_topk_kernel(tc, qT, k_words, k_scales, kn, qn, offs, ou
 
         q_raw = []
         for o in range(PASSES):
-            raw = sb.tile([P, 4, NQ], F32, name="q_raw%d" % o, align_bytes=64)
+            raw = sb.tile([P, 4, NQ], F32, name="q_raw%d" % o, tag="q_raw%d" % o, align_bytes=64)
             nc.sync.dma_start(raw[:], qT[0, 512 * o : 512 * (o + 1), :].rearrange("(p t) q -> p t q", t=4))
             q_raw.append(raw)
 
@@ -96,11 +96,12 @@ def tile_attend_infodist_topk_kernel(tc, qT, k_words, k_scales, kn, qn, offs, ou
         q_codes, q_planes = {}, {}
         for o, j in ((0, 0), (0, 1), (1, 0), (1, 1)):
             grouped = sb.tile([P, P, 4], BF16, name="grouped%d%d" % (o, j), align_bytes=64)
-            src = q_raw[o][:, :, P * j : P * (j + 1)].rearrange("p t m -> p m t")
-            if (o, j) == (1, 0):
-                nc.vector.tensor_copy(grouped[:], src)
+            src = q_raw[o][:, :, P * j : P * (j + 1)].rearrange("p t (c i) -> p c t i", i=4)
+            dst = grouped[:].rearrange("p (c i) t -> p c t i", i=4)
+            if o != j:
+                nc.vector.tensor_copy(dst, src)
             else:
-                nc.scalar.copy(grouped[:], src)
+                nc.scalar.copy(dst, src)
             codes = sb.tile([P, P], U32, name="q_codes%d%d" % (o, j), align_bytes=64)
             plane = sb.tile([P, P], U8, name="q_plane%d%d" % (o, j), align_bytes=64)
             nc.vector.quantize_mx(
@@ -108,41 +109,30 @@ def tile_attend_infodist_topk_kernel(tc, qT, k_words, k_scales, kn, qn, offs, ou
             )
             q_codes[(o, j)], q_planes[(o, j)] = codes, plane
 
-        kn_rows = sb.tile([P, N], F32, name="kn_rows", align_bytes=64)
+        kn_rows = sb.tile([P, N], F32, name="kn_rows", tag="q_raw1", align_bytes=64)
         nc.scalar.copy(kn_rows[:], kn_spread[:])
 
-        def product(acc, o, j, c0, c1):
-            nc.tensor.matmul_mx(
-                out=acc,
-                lhsT=q_codes[(o, j)][:].bitcast(FP8X4),
-                lhsT_scale=q_planes[(o, j)][:],
-                rhs=k_codes[o][:, 2 * c0 : 2 * c1].bitcast(FP4X4),
-                rhs_scale=k_planes[:].bitcast(U8)[:, N * o + c0 : N * o + c1],
-                start=(o == 0),
-                stop=(o == PASSES - 1),
-            )
-
-        def finish(acc, res, j, c0, c1):
-            part = sb.tile([P, c1 - c0], F32, name="part%d_%d" % (j, c0))
-            nc.vector.scalar_tensor_tensor(part[:], acc, -2.0, kn_rows[:, c0:c1], ALU.mult, ALU.add)
-            if j == 1 and c0 >= HALF:
-                nc.vector.tensor_scalar(res, part[:], qn_col[:, j : j + 1], 0.0, ALU.add, ALU.max)
-            else:
-                nc.scalar.activation(res, part[:], ACT.Relu, bias=qn_col[:, j : j + 1])
-
-        acc0 = ps.tile([P, N], F32, name="acc0")
-        acc1 = [ps.tile([P, P], F32, name="acc1_%d" % b) for b in range(4)]
+        acc = [ps.tile([P, N], F32, name="acc%d" % j) for j in range(QT)]
         for o in range(PASSES):
-            product(acc0[:], o, 0, 0, N)
-        for o in range(PASSES):
-            for b in range(4):
-                product(acc1[b][:], o, 1, P * b, P * (b + 1))
-        for h in range(2):
-            res = sb.tile([P, HALF], F32, name="res0_%d" % h)
-            finish(acc0[:, HALF * h : HALF * (h + 1)], res[:], 0, HALF * h, HALF * (h + 1))
-            nc.sync.dma_start(out[0, 0:P, HALF * h : HALF * (h + 1)], res[:])
-        for h in range(2):
-            res = sb.tile([P, HALF], F32, name="res1_%d" % h)
-            for b in (2 * h, 2 * h + 1):
-                finish(acc1[b][:], res[:, P * (b % 2) : P * (b % 2 + 1)], 1, P * b, P * (b + 1))
-            nc.sync.dma_start(out[0, P : 2 * P, HALF * h : HALF * (h + 1)], res[:])
+            for j in range(QT):
+                nc.tensor.matmul_mx(
+                    out=acc[j][:],
+                    lhsT=q_codes[(o, j)][:].bitcast(FP8X4),
+                    lhsT_scale=q_planes[(o, j)][:],
+                    rhs=k_codes[o][:].bitcast(FP4X4),
+                    rhs_scale=k_planes[:].bitcast(U8)[:, N * o : N * (o + 1)],
+                    start=(o == 0),
+                    stop=(o == PASSES - 1),
+                )
+
+        for j in range(QT):
+            for h in range(2):
+                cols = slice(HALF * h, HALF * (h + 1))
+                part = sb.tile([P, HALF], F32, name="part%d_%d" % (j, h))
+                res = sb.tile([P, HALF], F32, name="res%d_%d" % (j, h))
+                nc.vector.scalar_tensor_tensor(part[:], acc[j][:, cols], -2.0, kn_rows[:, cols], ALU.mult, ALU.add)
+                if (j, h) == (1, 1):
+                    nc.vector.tensor_scalar(res[:], part[:], qn_col[:, j : j + 1], 0.0, ALU.add, ALU.max)
+                else:
+                    nc.scalar.activation(res[:], part[:], ACT.Relu, bias=qn_col[:, j : j + 1])
+                nc.sync.dma_start(out[0, P * j : P * (j + 1), cols], res[:])

@@ -1,7 +1,6 @@
 from contextlib import ExitStack
 
 import concourse.mybir as mybir
-from concourse.masks import make_identity
 
 N, T, D, NQ = 512, 2048, 1024, 256
 FLOPS = 2 * NQ * N * D
@@ -22,6 +21,7 @@ P = 128
 PASSES = 2
 QT = 2
 HALF = N // 2
+KN_SPLIT = 1408
 
 
 def tile_attend_infodist_topk_kernel(tc, qT, k_words, k_scales, kn, qn, offs, out):
@@ -32,7 +32,7 @@ def tile_attend_infodist_topk_kernel(tc, qT, k_words, k_scales, kn, qn, offs, ou
 
         zero_col = sb.tile([P, 1], F32, name="zero_col")
         nc.vector.memset(zero_col[:], 0.0)
-        qn_rows = sb.tile([P, P], F32, name="qn_rows")
+        qn_rows = sb.tile([P, P], F32, name="qn_rows", tag="q_raw1", align_bytes=64)
         nc.scalar.copy(qn_rows[0 : P - QT, :], zero_col[0 : P - QT, :].to_broadcast([P - QT, P]))
 
         scale_win = sb.tile([P, T // 4], I32, name="scale_win", align_bytes=64)
@@ -47,24 +47,36 @@ def tile_attend_infodist_topk_kernel(tc, qT, k_words, k_scales, kn, qn, offs, ou
         word_win = sb.tile([P, T], I32, name="word_win", align_bytes=64)
         nc.sync.dma_start(word_win[:], k_words[0].rearrange("p t b -> p (t b)").bitcast(I32))
 
+        nc.scalar.dma_start(qn_rows[P - QT : P, :], qn[0].rearrange("(j p) o -> j (p o)", p=P))
+
+        k_planes = sb.tile([P, PASSES * N // 4], I32, name="k_planes", align_bytes=64)
+        nc.vector.memset(kn_win[0:127, 0:KN_SPLIT], 0.0)
+        nc.gpsimd.memset(kn_win[0:127, KN_SPLIT:T], 0.0)
+        nc.gpsimd.memset(k_planes[:], 0)
+
+        zeros = sb.tile([P, P], F32, name="zeros", tag="q_raw0", align_bytes=64)
+        ident = sb.tile([P, P], F32, name="ident")
+        nc.gpsimd.memset(zeros[:], 0.0)
+        nc.gpsimd.affine_select(
+            out=ident[:],
+            in_=zeros[:],
+            compare_op=ALU.not_equal,
+            fill=1.0,
+            base=0,
+            pattern=[[-1, P]],
+            channel_multiplier=1,
+        )
+        qn_turned = ps.tile([P, P], F32, name="qn_turned", tag="bank0")
+        nc.tensor.transpose(qn_turned[:], qn_rows[:], ident[:])
+        qn_col = sb.tile([P, QT], F32, name="qn_col")
+        nc.scalar.copy(qn_col[:], qn_turned[:, P - QT : P])
+
         q_raw = []
         for o in range(PASSES):
             raw = sb.tile([P, 4, NQ], F32, name="q_raw%d" % o, tag="q_raw%d" % o, align_bytes=64)
             nc.sync.dma_start(raw[:], qT[0, 512 * o : 512 * (o + 1), :].rearrange("(p t) q -> p t q", t=4))
             q_raw.append(raw)
 
-        nc.scalar.dma_start(qn_rows[P - QT : P, :], qn[0].rearrange("(j p) o -> j (p o)", p=P))
-
-        k_planes = sb.tile([P, PASSES * N // 4], I32, name="k_planes", align_bytes=64)
-        nc.vector.memset(kn_win[0:127, :], 0.0)
-        nc.vector.memset(k_planes[:], 0)
-
-        ident = sb.tile([P, P], F32, name="ident")
-        make_identity(nc, ident[:])
-        qn_turned = ps.tile([P, P], F32, name="qn_turned")
-        nc.tensor.transpose(qn_turned[:], qn_rows[:], ident[:])
-        qn_col = sb.tile([P, QT], F32, name="qn_col")
-        nc.scalar.copy(qn_col[:], qn_turned[:, P - QT : P])
 
         scale_g = sb.tile([P, N], U8, name="scale_g", align_bytes=64)
         nc.vector.tensor_copy(scale_g[:], scale_win[:].bitcast(U8).indirect(offsets[:]))
@@ -75,30 +87,39 @@ def tile_attend_infodist_topk_kernel(tc, qT, k_words, k_scales, kn, qn, offs, ou
             )
 
         kn_g = sb.tile([P, N], F32, name="kn_g", align_bytes=64)
-        nc.vector.tensor_copy(kn_g[:], kn_win[:].indirect(offsets[:]))
-        kn_turned = ps.tile([P, 4, P], F32, name="kn_turned")
+        for h in range(2):
+            nc.vector.tensor_copy(
+                kn_g[:, HALF * h : HALF * (h + 1)],
+                kn_win[:].indirect(offsets[:, HALF // 16 * h : HALF // 16 * (h + 1)]),
+            )
+        kn_turned = ps.tile([P, 4, P], F32, name="kn_turned", tag="bank1")
         for b in range(4):
             nc.tensor.transpose(kn_turned[:, b, :], kn_g[:, P * b : P * (b + 1)], ident[:])
         kn_col = sb.tile([P, 4], F32, name="kn_col")
         nc.scalar.copy(kn_col[:], kn_turned[:, :, P - 1])
-        kn_spread = ps.tile([P, N], F32, name="kn_spread")
+        kn_spread = ps.tile([P, N], F32, name="kn_spread", tag="bank7")
         for b in range(4):
             nc.tensor.transpose(kn_spread[:, P * b : P * (b + 1)], kn_col[:, b : b + 1].to_broadcast([P, P]), ident[:])
 
         word_g = sb.tile([P, N], U32, name="word_g", align_bytes=64)
-        nc.vector.tensor_copy(word_g[:], word_win[:].bitcast(U32).indirect(offsets[:]))
-        k_codes = []
-        for o in range(PASSES):
-            codes = sb.tile([P, 2 * N], U8, name="k_codes%d" % o, align_bytes=64)
-            nc.vector.tensor_copy(codes[:].bitcast(U16), word_g[:].bitcast(U16)[:, o : 2 * N : 2])
-            k_codes.append(codes)
+        for h in range(2):
+            nc.vector.tensor_copy(
+                word_g[:, HALF * h : HALF * (h + 1)],
+                word_win[:].bitcast(U32).indirect(offsets[:, HALF // 16 * h : HALF // 16 * (h + 1)]),
+            )
+        k_codes = sb.tile([P, PASSES, 2 * N], U8, name="k_codes", align_bytes=64)
+        for h in range(2):
+            nc.vector.tensor_copy(
+                k_codes[:].bitcast(U16)[:, :, HALF * h : HALF * (h + 1)],
+                word_g[:, HALF * h : HALF * (h + 1)].bitcast(U16).rearrange("p (n o) -> p o n", o=PASSES),
+            )
 
         q_codes, q_planes = {}, {}
         for o, j in ((0, 0), (0, 1), (1, 0), (1, 1)):
             grouped = sb.tile([P, P, 4], BF16, name="grouped%d%d" % (o, j), align_bytes=64)
             src = q_raw[o][:, :, P * j : P * (j + 1)].rearrange("p t (c i) -> p c t i", i=4)
             dst = grouped[:].rearrange("p (c i) t -> p c t i", i=4)
-            if o != j:
+            if (o, j) == (1, 0):
                 nc.vector.tensor_copy(dst, src)
             else:
                 nc.scalar.copy(dst, src)
@@ -109,30 +130,36 @@ def tile_attend_infodist_topk_kernel(tc, qT, k_words, k_scales, kn, qn, offs, ou
             )
             q_codes[(o, j)], q_planes[(o, j)] = codes, plane
 
-        kn_rows = sb.tile([P, N], F32, name="kn_rows", tag="q_raw1", align_bytes=64)
+        kn_rows = sb.tile([P, N], F32, name="kn_rows", tag="q_raw0", align_bytes=64)
         nc.scalar.copy(kn_rows[:], kn_spread[:])
 
-        acc = [ps.tile([P, N], F32, name="acc%d" % j) for j in range(QT)]
+        acc = [ps.tile([P, P], F32, name="acc%d" % g, tag="bank%d" % g) for g in range(4 * QT)]
         for o in range(PASSES):
-            for j in range(QT):
+            for g in range(4 * QT):
+                j, b = divmod(g, 4)
                 nc.tensor.matmul_mx(
-                    out=acc[j][:],
+                    out=acc[g][:],
                     lhsT=q_codes[(o, j)][:].bitcast(FP8X4),
                     lhsT_scale=q_planes[(o, j)][:],
-                    rhs=k_codes[o][:].bitcast(FP4X4),
-                    rhs_scale=k_planes[:].bitcast(U8)[:, N * o : N * (o + 1)],
+                    rhs=k_codes[:, o, 2 * P * b : 2 * P * (b + 1)].bitcast(FP4X4),
+                    rhs_scale=k_planes[:].bitcast(U8)[:, N * o + P * b : N * o + P * (b + 1)],
                     start=(o == 0),
                     stop=(o == PASSES - 1),
                 )
 
         for j in range(QT):
             for h in range(2):
-                cols = slice(HALF * h, HALF * (h + 1))
-                part = sb.tile([P, HALF], F32, name="part%d_%d" % (j, h))
                 res = sb.tile([P, HALF], F32, name="res%d_%d" % (j, h))
-                nc.vector.scalar_tensor_tensor(part[:], acc[j][:, cols], -2.0, kn_rows[:, cols], ALU.mult, ALU.add)
-                if (j, h) == (1, 1):
-                    nc.vector.tensor_scalar(res[:], part[:], qn_col[:, j : j + 1], 0.0, ALU.add, ALU.max)
-                else:
-                    nc.scalar.activation(res[:], part[:], ACT.Relu, bias=qn_col[:, j : j + 1])
-                nc.sync.dma_start(out[0, P * j : P * (j + 1), cols], res[:])
+                for e in range(2):
+                    b = 2 * h + e
+                    part = sb.tile([P, P], F32, name="part%d_%d" % (j, b))
+                    nc.vector.scalar_tensor_tensor(
+                        part[:], acc[4 * j + b][:], -2.0, kn_rows[:, P * b : P * (b + 1)], ALU.mult, ALU.add
+                    )
+                    if (j, b) == (1, 3):
+                        nc.vector.tensor_scalar(
+                            res[:, P * e : P * (e + 1)], part[:], qn_col[:, j : j + 1], 0.0, ALU.add, ALU.max
+                        )
+                    else:
+                        nc.scalar.activation(res[:, P * e : P * (e + 1)], part[:], ACT.Relu, bias=qn_col[:, j : j + 1])
+                nc.sync.dma_start(out[0, P * j : P * (j + 1), HALF * h : HALF * (h + 1)], res[:])

@@ -51,12 +51,11 @@ def tile_attend_infodist_topk_kernel(tc, qT, k_words, k_scales, kn, qn, offs, ou
 
         k_planes = sb.tile([P, PASSES * N // 4], I32, name="k_planes", align_bytes=64)
         nc.vector.memset(kn_win[0:127, 0:KN_SPLIT], 0.0)
-        nc.gpsimd.memset(kn_win[0:127, KN_SPLIT:T], 0.0)
-        nc.gpsimd.memset(k_planes[:], 0)
-
         zeros = sb.tile([P, P], F32, name="zeros", tag="q_raw0", align_bytes=64)
-        ident = sb.tile([P, P], F32, name="ident")
         nc.gpsimd.memset(zeros[:], 0.0)
+        nc.gpsimd.memset(kn_win[0:127, KN_SPLIT:T], 0.0)
+
+        ident = sb.tile([P, P], F32, name="ident")
         nc.gpsimd.affine_select(
             out=ident[:],
             in_=zeros[:],
@@ -66,6 +65,7 @@ def tile_attend_infodist_topk_kernel(tc, qT, k_words, k_scales, kn, qn, offs, ou
             pattern=[[-1, P]],
             channel_multiplier=1,
         )
+        nc.gpsimd.memset(k_planes[:], 0)
         qn_turned = ps.tile([P, P], F32, name="qn_turned", tag="bank0")
         nc.tensor.transpose(qn_turned[:], qn_rows[:], ident[:])
         qn_col = sb.tile([P, QT], F32, name="qn_col")
@@ -97,9 +97,11 @@ def tile_attend_infodist_topk_kernel(tc, qT, k_words, k_scales, kn, qn, offs, ou
             nc.tensor.transpose(kn_turned[:, b, :], kn_g[:, P * b : P * (b + 1)], ident[:])
         kn_col = sb.tile([P, 4], F32, name="kn_col")
         nc.scalar.copy(kn_col[:], kn_turned[:, :, P - 1])
-        kn_spread = ps.tile([P, N], F32, name="kn_spread", tag="bank7")
+        kn_spread = [ps.tile([P, HALF], F32, name="kn_spread%d" % h, tag="bank%d" % (6 + h)) for h in range(2)]
         for b in range(4):
-            nc.tensor.transpose(kn_spread[:, P * b : P * (b + 1)], kn_col[:, b : b + 1].to_broadcast([P, P]), ident[:])
+            nc.tensor.transpose(
+                kn_spread[b // 2][:, P * (b % 2) : P * (b % 2 + 1)], kn_col[:, b : b + 1].to_broadcast([P, P]), ident[:]
+            )
 
         word_g = sb.tile([P, N], U32, name="word_g", align_bytes=64)
         for h in range(2):
@@ -116,7 +118,7 @@ def tile_attend_infodist_topk_kernel(tc, qT, k_words, k_scales, kn, qn, offs, ou
 
         q_codes, q_planes = {}, {}
         for o, j in ((0, 0), (0, 1), (1, 0), (1, 1)):
-            grouped = sb.tile([P, P, 4], BF16, name="grouped%d%d" % (o, j), align_bytes=64)
+            grouped = sb.tile([P, P, 4], BF16, name="grouped%d%d" % (o, j), tag="grouped%d%d" % (o, j), align_bytes=64)
             src = q_raw[o][:, :, P * j : P * (j + 1)].rearrange("p t (c i) -> p c t i", i=4)
             dst = grouped[:].rearrange("p (c i) t -> p c t i", i=4)
             if (o, j) == (1, 0):
@@ -130,12 +132,15 @@ def tile_attend_infodist_topk_kernel(tc, qT, k_words, k_scales, kn, qn, offs, ou
             )
             q_codes[(o, j)], q_planes[(o, j)] = codes, plane
 
-        kn_rows = sb.tile([P, N], F32, name="kn_rows", tag="q_raw0", align_bytes=64)
-        nc.scalar.copy(kn_rows[:], kn_spread[:])
+        kn_lo = sb.tile([P, HALF], F32, name="kn_lo", tag="grouped01", align_bytes=64)
+        nc.vector.tensor_copy(kn_lo[:], kn_spread[0][:])
+        kn_hi = sb.tile([P, HALF], F32, name="kn_hi", tag="q_raw1", align_bytes=64)
+        nc.scalar.copy(kn_hi[:], kn_spread[1][:])
+        kn_rows = (kn_lo, kn_hi)
 
         acc = [ps.tile([P, P], F32, name="acc%d" % g, tag="bank%d" % g) for g in range(4 * QT)]
-        for o in range(PASSES):
-            for g in range(4 * QT):
+        for o, groups in ((0, range(0, 6)), (1, range(0, 4)), (0, range(6, 8)), (1, range(4, 8))):
+            for g in groups:
                 j, b = divmod(g, 4)
                 nc.tensor.matmul_mx(
                     out=acc[g][:],
@@ -154,7 +159,7 @@ def tile_attend_infodist_topk_kernel(tc, qT, k_words, k_scales, kn, qn, offs, ou
                     b = 2 * h + e
                     part = sb.tile([P, P], F32, name="part%d_%d" % (j, b))
                     nc.vector.scalar_tensor_tensor(
-                        part[:], acc[4 * j + b][:], -2.0, kn_rows[:, P * b : P * (b + 1)], ALU.mult, ALU.add
+                        part[:], acc[4 * j + b][:], -2.0, kn_rows[h][:, P * e : P * (e + 1)], ALU.mult, ALU.add
                     )
                     if (j, b) == (1, 3):
                         nc.vector.tensor_scalar(

@@ -21,7 +21,6 @@ P = 128
 PASSES = 2
 QT = 2
 HALF = N // 2
-KN_SPLIT = 1408
 
 
 def tile_attend_infodist_topk_kernel(tc, qT, k_words, k_scales, kn, qn, offs, out):
@@ -50,10 +49,9 @@ def tile_attend_infodist_topk_kernel(tc, qT, k_words, k_scales, kn, qn, offs, ou
         nc.scalar.dma_start(qn_rows[P - QT : P, :], qn[0].rearrange("(j p) o -> j (p o)", p=P))
 
         k_planes = sb.tile([P, PASSES * N // 4], I32, name="k_planes", align_bytes=64)
-        nc.vector.memset(kn_win[0:127, 0:KN_SPLIT], 0.0)
+        nc.vector.memset(kn_win[0:127, :], 0.0)
         zeros = sb.tile([P, P], F32, name="zeros", tag="q_raw0", align_bytes=64)
         nc.gpsimd.memset(zeros[:], 0.0)
-        nc.gpsimd.memset(kn_win[0:127, KN_SPLIT:T], 0.0)
 
         ident = sb.tile([P, P], F32, name="ident")
         nc.gpsimd.affine_select(

@@ -21,37 +21,45 @@ P = 128
 PASSES = 2
 QT = 2
 HALF = N // 2
+SLOT = 1024
 
 
 def tile_attend_infodist_topk_kernel(tc, qT, k_words, k_scales, kn, qn, offs, out):
     nc = tc.nc
     with ExitStack() as ctx:
         sb = ctx.enter_context(tc.tile_pool(name="sb", bufs=1))
+        shared = ctx.enter_context(tc.tile_pool(name="shared", bufs=1))
         ps = ctx.enter_context(tc.psum_pool(name="ps", bufs=1))
 
         zero_col = sb.tile([P, 1], F32, name="zero_col")
-        nc.vector.memset(zero_col[:], 0.0)
-        qn_rows = sb.tile([P, P], F32, name="qn_rows", tag="q_raw1", align_bytes=64)
-        nc.scalar.copy(qn_rows[0 : P - QT, :], zero_col[0 : P - QT, :].to_broadcast([P - QT, P]))
+        nc.gpsimd.memset(zero_col[:], 0.0)
+        zeros = sb.tile([P, P], F32, name="zeros", tag="planes", align_bytes=64)
+        nc.scalar.copy(zeros[:], zero_col[:].to_broadcast([P, P]))
 
         scale_win = sb.tile([P, T // 4], I32, name="scale_win", align_bytes=64)
         nc.sync.dma_start(scale_win[96:128, :], k_scales.bitcast(I32).rearrange("o f w -> f o w"))
         offsets = sb.tile([P, N // 16], U16, name="offsets")
         nc.sync.dma_start(offsets[:], offs)
-        nc.vector.memset(scale_win[0:96, :], 0)
+        nc.gpsimd.memset(scale_win[0:96, :], 0)
 
-        kn_win = sb.tile([P, T], F32, name="kn_win", align_bytes=64)
+        kn_win = sb.tile([P, T], F32, name="kn_win", tag="kn_win", align_bytes=64)
         nc.sync.dma_start(kn_win[127:128, :], kn[0:1, :])
 
         word_win = sb.tile([P, T], I32, name="word_win", align_bytes=64)
         nc.sync.dma_start(word_win[:], k_words[0].rearrange("p t b -> p (t b)").bitcast(I32))
 
-        nc.scalar.dma_start(qn_rows[P - QT : P, :], qn[0].rearrange("(j p) o -> j (p o)", p=P))
+        q_first = sb.tile([P, 4, NQ], F32, name="q_first", align_bytes=64)
+        nc.sync.dma_start(q_first[:], qT[0, 0:512, :].rearrange("(p t) q -> p t q", t=4))
+        q_raw = {(0, j): q_first[:, :, P * j : P * (j + 1)] for j in range(QT)}
 
-        k_planes = sb.tile([P, PASSES * N // 4], I32, name="k_planes", align_bytes=64)
+        def load_last(j, tag):
+            raw = sb.tile([P, 4, P], F32, name="q_last%d" % j, tag=tag, align_bytes=64)
+            nc.sync.dma_start(raw[:], qT[0, 512:1024, P * j : P * (j + 1)].rearrange("(p t) q -> p t q", t=4))
+            q_raw[(1, j)] = raw[:]
+
+        load_last(0, "q_last0")
+
         nc.vector.memset(kn_win[0:127, :], 0.0)
-        zeros = sb.tile([P, P], F32, name="zeros", tag="q_raw0", align_bytes=64)
-        nc.gpsimd.memset(zeros[:], 0.0)
 
         ident = sb.tile([P, P], F32, name="ident")
         nc.gpsimd.affine_select(
@@ -63,18 +71,11 @@ def tile_attend_infodist_topk_kernel(tc, qT, k_words, k_scales, kn, qn, offs, ou
             pattern=[[-1, P]],
             channel_multiplier=1,
         )
+        k_planes = sb.tile([P, PASSES * N // 4], I32, name="k_planes", tag="planes", align_bytes=64)
         nc.gpsimd.memset(k_planes[:], 0)
-        qn_turned = ps.tile([P, P], F32, name="qn_turned", tag="bank0")
-        nc.tensor.transpose(qn_turned[:], qn_rows[:], ident[:])
-        qn_col = sb.tile([P, QT], F32, name="qn_col")
-        nc.scalar.copy(qn_col[:], qn_turned[:, P - QT : P])
 
-        q_raw = []
-        for o in range(PASSES):
-            raw = sb.tile([P, 4, NQ], F32, name="q_raw%d" % o, tag="q_raw%d" % o, align_bytes=64)
-            nc.sync.dma_start(raw[:], qT[0, 512 * o : 512 * (o + 1), :].rearrange("(p t) q -> p t q", t=4))
-            q_raw.append(raw)
-
+        kn_g = shared.tile([P, 3 * SLOT // 4], F32, name="kn_g", offset=0, align_bytes=64)
+        nc.scalar.activation(kn_g[:, 0:HALF], kn_win[:].indirect(offsets[:, 0 : HALF // 16]), ACT.Copy)
 
         scale_g = sb.tile([P, N], U8, name="scale_g", align_bytes=64)
         nc.vector.tensor_copy(scale_g[:], scale_win[:].bitcast(U8).indirect(offsets[:]))
@@ -84,22 +85,22 @@ def tile_attend_infodist_topk_kernel(tc, qT, k_words, k_scales, kn, qn, offs, ou
                 scale_g[:].bitcast(I32)[96 + 8 * quad : 96 + 8 * quad + 8, :],
             )
 
-        kn_g = sb.tile([P, N], F32, name="kn_g", align_bytes=64)
-        for h in range(2):
-            nc.vector.tensor_copy(
-                kn_g[:, HALF * h : HALF * (h + 1)],
-                kn_win[:].indirect(offsets[:, HALF // 16 * h : HALF // 16 * (h + 1)]),
-            )
-        kn_turned = ps.tile([P, 4, P], F32, name="kn_turned", tag="bank1")
+        nc.vector.tensor_copy(kn_g[:, HALF:N], kn_win[:].indirect(offsets[:, HALF // 16 : N // 16]))
+        load_last(1, "kn_win")
+        kn_turned = ps.tile([P, 4, P], F32, name="kn_turned", tag="bank6")
         for b in range(4):
             nc.tensor.transpose(kn_turned[:, b, :], kn_g[:, P * b : P * (b + 1)], ident[:])
-        kn_col = sb.tile([P, 4], F32, name="kn_col")
+        kn_col = sb.tile([P, 4], F32, name="kn_col", tag="kn_col")
         nc.scalar.copy(kn_col[:], kn_turned[:, :, P - 1])
-        kn_spread = [ps.tile([P, HALF], F32, name="kn_spread%d" % h, tag="bank%d" % (6 + h)) for h in range(2)]
+        kn_spread = [ps.tile([P, HALF], F32, name="kn_spread%d" % h, tag="bank%d" % (4 + h)) for h in range(2)]
         for b in range(4):
             nc.tensor.transpose(
                 kn_spread[b // 2][:, P * (b % 2) : P * (b % 2 + 1)], kn_col[:, b : b + 1].to_broadcast([P, P]), ident[:]
             )
+
+        qn_col = sb.tile([P, QT], F32, name="qn_col", tag="kn_col")
+        with nc.allow_non_contiguous_dma(reason="one number a partition and query tile"):
+            nc.sync.dma_start(qn_col[:], qn[0].rearrange("(j p) o -> p (j o)", p=P))
 
         word_g = sb.tile([P, N], U32, name="word_g", align_bytes=64)
         for h in range(2):
@@ -114,15 +115,17 @@ def tile_attend_infodist_topk_kernel(tc, qT, k_words, k_scales, kn, qn, offs, ou
                 word_g[:, HALF * h : HALF * (h + 1)].bitcast(U16).rearrange("p (n o) -> p o n", o=PASSES),
             )
 
+        def interleave(o, j, slot, on_vector):
+            grouped = shared.tile([P, P, 4], BF16, name="grouped%d%d" % (o, j), offset=slot * SLOT, align_bytes=64)
+            for lo, hi, copy in ((0, P - on_vector, nc.scalar.copy), (P - on_vector, P, nc.vector.tensor_copy)):
+                if hi > lo:
+                    src = q_raw[(o, j)][:, :, lo:hi].rearrange("p t (c i) -> p c t i", i=4)
+                    copy(grouped[:, lo:hi, :].rearrange("p (c i) t -> p c t i", i=4), src)
+            return grouped
+
         q_codes, q_planes = {}, {}
-        for o, j in ((0, 0), (0, 1), (1, 0), (1, 1)):
-            grouped = sb.tile([P, P, 4], BF16, name="grouped%d%d" % (o, j), tag="grouped%d%d" % (o, j), align_bytes=64)
-            src = q_raw[o][:, :, P * j : P * (j + 1)].rearrange("p t (c i) -> p c t i", i=4)
-            dst = grouped[:].rearrange("p (c i) t -> p c t i", i=4)
-            if (o, j) == (1, 0):
-                nc.vector.tensor_copy(dst, src)
-            else:
-                nc.scalar.copy(dst, src)
+
+        def quantise(o, j, grouped):
             codes = sb.tile([P, P], U32, name="q_codes%d%d" % (o, j), align_bytes=64)
             plane = sb.tile([P, P], U8, name="q_plane%d%d" % (o, j), align_bytes=64)
             nc.vector.quantize_mx(
@@ -130,39 +133,49 @@ def tile_attend_infodist_topk_kernel(tc, qT, k_words, k_scales, kn, qn, offs, ou
             )
             q_codes[(o, j)], q_planes[(o, j)] = codes, plane
 
-        kn_lo = sb.tile([P, HALF], F32, name="kn_lo", tag="grouped01", align_bytes=64)
-        nc.vector.tensor_copy(kn_lo[:], kn_spread[0][:])
-        kn_hi = sb.tile([P, HALF], F32, name="kn_hi", tag="q_raw1", align_bytes=64)
+        quantise(0, 0, interleave(0, 0, 0, 0))
+        g10 = interleave(1, 0, 1, 0)
+        g01 = interleave(0, 1, 0, P)
+        quantise(1, 0, g10)
+        quantise(0, 1, g01)
+        kn_lo = sb.tile([P, HALF], F32, name="kn_lo", align_bytes=64)
+        nc.scalar.copy(kn_lo[:], kn_spread[0][:])
+        quantise(1, 1, interleave(1, 1, 2, 0))
+        kn_hi = sb.tile([P, HALF], F32, name="kn_hi", align_bytes=64)
         nc.scalar.copy(kn_hi[:], kn_spread[1][:])
         kn_rows = (kn_lo, kn_hi)
 
-        acc = [ps.tile([P, P], F32, name="acc%d" % g, tag="bank%d" % g) for g in range(4 * QT)]
-        for o, groups in ((0, range(0, 6)), (1, range(0, 4)), (0, range(6, 8)), (1, range(4, 8))):
-            for g in groups:
-                j, b = divmod(g, 4)
-                nc.tensor.matmul_mx(
-                    out=acc[g][:],
-                    lhsT=q_codes[(o, j)][:].bitcast(FP8X4),
-                    lhsT_scale=q_planes[(o, j)][:],
-                    rhs=k_codes[:, o, 2 * P * b : 2 * P * (b + 1)].bitcast(FP4X4),
-                    rhs_scale=k_planes[:].bitcast(U8)[:, N * o + P * b : N * o + P * (b + 1)],
-                    start=(o == 0),
-                    stop=(o == PASSES - 1),
-                )
+        def one_pass(o, g):
+            j, c, w = sums[g]
+            nc.tensor.matmul_mx(
+                out=acc[g][:],
+                lhsT=q_codes[(o, j)][:].bitcast(FP8X4),
+                lhsT_scale=q_planes[(o, j)][:],
+                rhs=k_codes[:, o, 2 * c : 2 * (c + w)].bitcast(FP4X4),
+                rhs_scale=k_planes[:].bitcast(U8)[:, N * o + c : N * o + c + w],
+                start=(o == 0),
+                stop=(o == PASSES - 1),
+            )
 
-        for j in range(QT):
-            for h in range(2):
-                res = sb.tile([P, HALF], F32, name="res%d_%d" % (j, h))
-                for e in range(2):
-                    b = 2 * h + e
-                    part = sb.tile([P, P], F32, name="part%d_%d" % (j, b))
-                    nc.vector.scalar_tensor_tensor(
-                        part[:], acc[4 * j + b][:], -2.0, kn_rows[h][:, P * e : P * (e + 1)], ALU.mult, ALU.add
-                    )
-                    if (j, b) == (1, 3):
-                        nc.vector.tensor_scalar(
-                            res[:, P * e : P * (e + 1)], part[:], qn_col[:, j : j + 1], 0.0, ALU.add, ALU.max
-                        )
-                    else:
-                        nc.scalar.activation(res[:, P * e : P * (e + 1)], part[:], ACT.Relu, bias=qn_col[:, j : j + 1])
-                nc.sync.dma_start(out[0, P * j : P * (j + 1), HALF * h : HALF * (h + 1)], res[:])
+        sums = [(0, 0, P), (0, P, P), (0, HALF, HALF), (1, 0, HALF), (1, HALF, P), (1, HALF + P, P)]
+        acc = [ps.tile([P, sums[g][2]], F32, name="acc%d" % g, tag="bank%d" % g) for g in range(len(sums))]
+        for groups in (range(0, 3), range(3, 4), range(4, 5), range(5, 6)):
+            for o in range(PASSES):
+                for g in groups:
+                    one_pass(o, g)
+
+        res = {}
+        for g, (j, c, w) in enumerate(sums):
+            h, lo = divmod(c, HALF)
+            if lo == 0:
+                res[(j, h)] = sb.tile([P, HALF], F32, name="res%d_%d" % (j, h))
+            part = sb.tile([P, w], F32, name="part%d" % g)
+            nc.vector.scalar_tensor_tensor(part[:], acc[g][:], -2.0, kn_rows[h][:, lo : lo + w], ALU.mult, ALU.add)
+            if g == len(sums) - 1:
+                nc.vector.tensor_scalar(
+                    res[(j, h)][:, lo : lo + w], part[:], qn_col[:, j : j + 1], 0.0, ALU.add, ALU.max
+                )
+            else:
+                nc.scalar.activation(res[(j, h)][:, lo : lo + w], part[:], ACT.Relu, bias=qn_col[:, j : j + 1])
+            if lo + w == HALF:
+                nc.sync.dma_start(out[0, P * j : P * (j + 1), HALF * h : HALF * (h + 1)], res[(j, h)][:])

@@ -32,15 +32,18 @@ def tile_attend_infodist_topk_kernel(tc, qT, k_words, k_scales, kn, qn, offs, ou
         ps = ctx.enter_context(tc.psum_pool(name="ps", bufs=1))
 
         zero_col = sb.tile([P, 1], F32, name="zero_col")
-        nc.gpsimd.memset(zero_col[:], 0.0)
+        nc.vector.memset(zero_col[:], 0.0)
+        qn_rows = sb.tile([P, P], F32, name="qn_rows", align_bytes=64)
+        nc.scalar.dma_start(qn_rows[P - QT : P, :], qn[0].rearrange("(j p) o -> j (p o)", p=P))
+        nc.scalar.copy(qn_rows[0 : P - QT, :], zero_col[0 : P - QT, :].to_broadcast([P - QT, P]))
         zeros = sb.tile([P, P], F32, name="zeros", tag="planes", align_bytes=64)
-        nc.scalar.copy(zeros[:], zero_col[:].to_broadcast([P, P]))
+        nc.gpsimd.memset(zeros[:], 0.0)
 
         scale_win = sb.tile([P, T // 4], I32, name="scale_win", align_bytes=64)
         nc.sync.dma_start(scale_win[96:128, :], k_scales.bitcast(I32).rearrange("o f w -> f o w"))
         offsets = sb.tile([P, N // 16], U16, name="offsets")
         nc.sync.dma_start(offsets[:], offs)
-        nc.gpsimd.memset(scale_win[0:96, :], 0)
+        nc.vector.memset(scale_win[0:96, :], 0)
 
         kn_win = sb.tile([P, T], F32, name="kn_win", tag="kn_win", align_bytes=64)
         nc.sync.dma_start(kn_win[127:128, :], kn[0:1, :])
@@ -74,6 +77,11 @@ def tile_attend_infodist_topk_kernel(tc, qT, k_words, k_scales, kn, qn, offs, ou
         k_planes = sb.tile([P, PASSES * N // 4], I32, name="k_planes", tag="planes", align_bytes=64)
         nc.gpsimd.memset(k_planes[:], 0)
 
+        qn_turned = ps.tile([P, P], F32, name="qn_turned", tag="bank7")
+        nc.tensor.transpose(qn_turned[:], qn_rows[:], ident[:])
+        qn_col = sb.tile([P, QT], F32, name="qn_col")
+        nc.scalar.copy(qn_col[:], qn_turned[:, P - QT : P])
+
         kn_g = shared.tile([P, 3 * SLOT // 4], F32, name="kn_g", offset=0, align_bytes=64)
         nc.scalar.activation(kn_g[:, 0:HALF], kn_win[:].indirect(offsets[:, 0 : HALF // 16]), ACT.Copy)
 
@@ -90,17 +98,13 @@ def tile_attend_infodist_topk_kernel(tc, qT, k_words, k_scales, kn, qn, offs, ou
         kn_turned = ps.tile([P, 4, P], F32, name="kn_turned", tag="bank6")
         for b in range(4):
             nc.tensor.transpose(kn_turned[:, b, :], kn_g[:, P * b : P * (b + 1)], ident[:])
-        kn_col = sb.tile([P, 4], F32, name="kn_col", tag="kn_col")
+        kn_col = sb.tile([P, 4], F32, name="kn_col")
         nc.scalar.copy(kn_col[:], kn_turned[:, :, P - 1])
         kn_spread = [ps.tile([P, HALF], F32, name="kn_spread%d" % h, tag="bank%d" % (4 + h)) for h in range(2)]
         for b in range(4):
             nc.tensor.transpose(
                 kn_spread[b // 2][:, P * (b % 2) : P * (b % 2 + 1)], kn_col[:, b : b + 1].to_broadcast([P, P]), ident[:]
             )
-
-        qn_col = sb.tile([P, QT], F32, name="qn_col", tag="kn_col")
-        with nc.allow_non_contiguous_dma(reason="one number a partition and query tile"):
-            nc.sync.dma_start(qn_col[:], qn[0].rearrange("(j p) o -> p (j o)", p=P))
 
         word_g = sb.tile([P, N], U32, name="word_g", align_bytes=64)
         for h in range(2):

@@ -77,12 +77,12 @@ def tile_attend_infodist_topk_kernel(tc, qT, k_words, k_scales, kn, qn, offs, ou
         k_planes = sb.tile([P, PASSES * N // 4], I32, name="k_planes", tag="planes", align_bytes=64)
         nc.gpsimd.memset(k_planes[:], 0)
 
-        qn_turned = ps.tile([P, P], F32, name="qn_turned", tag="bank7")
+        qn_turned = ps.tile([P, P], F32, name="qn_turned", tag="bank5")
         nc.tensor.transpose(qn_turned[:], qn_rows[:], ident[:])
         qn_col = sb.tile([P, QT], F32, name="qn_col")
         nc.scalar.copy(qn_col[:], qn_turned[:, P - QT : P])
 
-        kn_g = shared.tile([P, 3 * SLOT // 4], F32, name="kn_g", offset=0, align_bytes=64)
+        kn_g = shared.tile([P, N], F32, name="kn_g", offset=0, align_bytes=64)
         nc.scalar.activation(kn_g[:, 0:HALF], kn_win[:].indirect(offsets[:, 0 : HALF // 16]), ACT.Copy)
 
         scale_g = sb.tile([P, N], U8, name="scale_g", align_bytes=64)
@@ -95,12 +95,12 @@ def tile_attend_infodist_topk_kernel(tc, qT, k_words, k_scales, kn, qn, offs, ou
 
         nc.vector.tensor_copy(kn_g[:, HALF:N], kn_win[:].indirect(offsets[:, HALF // 16 : N // 16]))
         load_last(1, "kn_win")
-        kn_turned = ps.tile([P, 4, P], F32, name="kn_turned", tag="bank6")
+        kn_turned = ps.tile([P, 4, P], F32, name="kn_turned", tag="bank4")
         for b in range(4):
             nc.tensor.transpose(kn_turned[:, b, :], kn_g[:, P * b : P * (b + 1)], ident[:])
-        kn_col = sb.tile([P, 4], F32, name="kn_col")
-        nc.scalar.copy(kn_col[:], kn_turned[:, :, P - 1])
-        kn_spread = [ps.tile([P, HALF], F32, name="kn_spread%d" % h, tag="bank%d" % (4 + h)) for h in range(2)]
+        kn_col = shared.tile([P, 3 * SLOT // 4], F32, name="kn_col", offset=SLOT, align_bytes=64)
+        nc.scalar.copy(kn_col[:, 0:4], kn_turned[:, :, P - 1])
+        kn_spread = [ps.tile([P, HALF], F32, name="kn_spread%d" % h, tag="bank%d" % (6 + h)) for h in range(2)]
         for b in range(4):
             nc.tensor.transpose(
                 kn_spread[b // 2][:, P * (b % 2) : P * (b % 2 + 1)], kn_col[:, b : b + 1].to_broadcast([P, P]), ident[:]
@@ -138,15 +138,15 @@ def tile_attend_infodist_topk_kernel(tc, qT, k_words, k_scales, kn, qn, offs, ou
             q_codes[(o, j)], q_planes[(o, j)] = codes, plane
 
         quantise(0, 0, interleave(0, 0, 0, 0))
-        g10 = interleave(1, 0, 1, 0)
-        g01 = interleave(0, 1, 0, P)
-        quantise(1, 0, g10)
-        quantise(0, 1, g01)
         kn_lo = sb.tile([P, HALF], F32, name="kn_lo", align_bytes=64)
         nc.scalar.copy(kn_lo[:], kn_spread[0][:])
-        quantise(1, 1, interleave(1, 1, 2, 0))
-        kn_hi = sb.tile([P, HALF], F32, name="kn_hi", align_bytes=64)
+        g10 = interleave(1, 0, 1, P // 2)
+        g01 = interleave(0, 1, 2, P)
+        kn_hi = shared.tile([P, HALF], F32, name="kn_hi", offset=3 * SLOT, align_bytes=64)
         nc.scalar.copy(kn_hi[:], kn_spread[1][:])
+        quantise(1, 0, g10)
+        quantise(0, 1, g01)
+        quantise(1, 1, interleave(1, 1, 1, P // 2))
         kn_rows = (kn_lo, kn_hi)
 
         def one_pass(o, g):
@@ -161,25 +161,24 @@ def tile_attend_infodist_topk_kernel(tc, qT, k_words, k_scales, kn, qn, offs, ou
                 stop=(o == PASSES - 1),
             )
 
-        sums = [(0, 0, P), (0, P, P), (0, HALF, HALF), (1, 0, HALF), (1, HALF, P), (1, HALF + P, P)]
+        sums = [(j, P * b, P) for j in range(QT) for b in range(4)]
         acc = [ps.tile([P, sums[g][2]], F32, name="acc%d" % g, tag="bank%d" % g) for g in range(len(sums))]
-        for groups in (range(0, 3), range(3, 4), range(4, 5), range(5, 6)):
+        for groups in (range(0, 4), range(4, 6), range(6, 7), range(7, 8)):
             for o in range(PASSES):
                 for g in groups:
                     one_pass(o, g)
 
-        res = {}
+        res, part = {}, {}
         for g, (j, c, w) in enumerate(sums):
             h, lo = divmod(c, HALF)
             if lo == 0:
                 res[(j, h)] = sb.tile([P, HALF], F32, name="res%d_%d" % (j, h))
-            part = sb.tile([P, w], F32, name="part%d" % g)
-            nc.vector.scalar_tensor_tensor(part[:], acc[g][:], -2.0, kn_rows[h][:, lo : lo + w], ALU.mult, ALU.add)
-            if g == len(sums) - 1:
-                nc.vector.tensor_scalar(
-                    res[(j, h)][:, lo : lo + w], part[:], qn_col[:, j : j + 1], 0.0, ALU.add, ALU.max
-                )
-            else:
-                nc.scalar.activation(res[(j, h)][:, lo : lo + w], part[:], ACT.Relu, bias=qn_col[:, j : j + 1])
+                part[(j, h)] = sb.tile([P, HALF], F32, name="part%d_%d" % (j, h))
+            mine = part[(j, h)][:, lo : lo + w]
+            nc.vector.scalar_tensor_tensor(mine, acc[g][:], -2.0, kn_rows[h][:, lo : lo + w], ALU.mult, ALU.add)
+            if (j, h) != (1, 1):
+                nc.scalar.activation(res[(j, h)][:, lo : lo + w], mine, ACT.Relu, bias=qn_col[:, j : j + 1])
+            elif lo + w == HALF:
+                nc.vector.tensor_scalar(res[(j, h)][:], part[(j, h)][:], qn_col[:, j : j + 1], 0.0, ALU.add, ALU.max)
             if lo + w == HALF:
                 nc.sync.dma_start(out[0, P * j : P * (j + 1), HALF * h : HALF * (h + 1)], res[(j, h)][:])

@@ -20,6 +20,7 @@ ACT = mybir.ActivationFunctionType
 P = 128
 PASSES = 2
 QT = 2
+GROUPS = N // P
 HALF = N // 2
 SLOT = 1024
 
@@ -31,40 +32,47 @@ def tile_attend_infodist_topk_kernel(tc, qT, k_words, k_scales, kn, qn, offs, ou
         shared = ctx.enter_context(tc.tile_pool(name="shared", bufs=1))
         ps = ctx.enter_context(tc.psum_pool(name="ps", bufs=1))
 
+        def placed(shape, dtype, name, slot):
+            return shared.tile(shape, dtype, name=name, offset=int(slot * SLOT), align_bytes=64)
+
         zero_col = sb.tile([P, 1], F32, name="zero_col")
         nc.vector.memset(zero_col[:], 0.0)
         qn_rows = sb.tile([P, P], F32, name="qn_rows", align_bytes=64)
         nc.scalar.dma_start(qn_rows[P - QT : P, :], qn[0].rearrange("(j p) o -> j (p o)", p=P))
         nc.scalar.copy(qn_rows[0 : P - QT, :], zero_col[0 : P - QT, :].to_broadcast([P - QT, P]))
-        zeros = sb.tile([P, P], F32, name="zeros", tag="planes", align_bytes=64)
+        zeros = sb.tile([P, P], F32, name="zeros", align_bytes=64)
         nc.gpsimd.memset(zeros[:], 0.0)
 
-        scale_win = sb.tile([P, T // 4], I32, name="scale_win", align_bytes=64)
+        scale_win = placed([P, T // 4], I32, "scale_win", 0)
         nc.sync.dma_start(scale_win[96:128, :], k_scales.bitcast(I32).rearrange("o f w -> f o w"))
         offsets = sb.tile([P, N // 16], U16, name="offsets")
         nc.sync.dma_start(offsets[:], offs)
-        nc.vector.memset(scale_win[0:96, :], 0)
-
-        kn_win = sb.tile([P, T], F32, name="kn_win", tag="kn_win", align_bytes=64)
+        kn_win = placed([P, T], F32, "kn_win", 4)
         nc.sync.dma_start(kn_win[127:128, :], kn[0:1, :])
-
-        word_win = sb.tile([P, T], I32, name="word_win", align_bytes=64)
+        word_win = placed([P, T], I32, "word_win", 12)
         nc.sync.dma_start(word_win[:], k_words[0].rearrange("p t b -> p (t b)").bitcast(I32))
 
-        q_first = sb.tile([P, 4, NQ], F32, name="q_first", align_bytes=64)
-        nc.sync.dma_start(q_first[:], qT[0, 0:512, :].rearrange("(p t) q -> p t q", t=4))
+        def load_pass(o, slot):
+            raw = placed([P, 4, NQ], F32, "q_raw%d" % o, slot)
+            nc.sync.dma_start(raw[:], qT[0, 512 * o : 512 * (o + 1), :].rearrange("(p t) q -> p t q", t=4))
+            return raw
+
+        q_first = load_pass(0, 20)
         q_raw = {(0, j): q_first[:, :, P * j : P * (j + 1)] for j in range(QT)}
 
-        def load_last(j, tag):
-            raw = sb.tile([P, 4, P], F32, name="q_last%d" % j, tag=tag, align_bytes=64)
+        def load_last(j, slot):
+            raw = placed([P, 4, P], F32, "q_last%d" % j, slot)
             nc.sync.dma_start(raw[:], qT[0, 512:1024, P * j : P * (j + 1)].rearrange("(p t) q -> p t q", t=4))
             q_raw[(1, j)] = raw[:]
 
-        load_last(0, "q_last0")
+        load_last(0, 2)
 
-        nc.vector.memset(kn_win[0:127, :], 0.0)
+        nc.vector.memset(scale_win[0:96, :], 0)
+        k_planes = sb.tile([P, PASSES * N // 4], I32, name="k_planes", align_bytes=64)
+        nc.vector.memset(k_planes[:], 0)
+        nc.vector.memset(kn_win[0:127, 0 : 2048], 0.0)
 
-        ident = sb.tile([P, P], F32, name="ident")
+        ident = placed([P, P], F32, "ident", 28)
         nc.gpsimd.affine_select(
             out=ident[:],
             in_=zeros[:],
@@ -74,111 +82,115 @@ def tile_attend_infodist_topk_kernel(tc, qT, k_words, k_scales, kn, qn, offs, ou
             pattern=[[-1, P]],
             channel_multiplier=1,
         )
-        k_planes = sb.tile([P, PASSES * N // 4], I32, name="k_planes", tag="planes", align_bytes=64)
-        nc.gpsimd.memset(k_planes[:], 0)
 
-        qn_turned = ps.tile([P, P], F32, name="qn_turned", tag="bank5")
+        qn_turned = ps.tile([P, P], F32, name="qn_turned", tag="bank0")
         nc.tensor.transpose(qn_turned[:], qn_rows[:], ident[:])
-        qn_col = sb.tile([P, QT], F32, name="qn_col")
-        nc.scalar.copy(qn_col[:], qn_turned[:, P - QT : P])
 
-        kn_g = shared.tile([P, N], F32, name="kn_g", offset=0, align_bytes=64)
-        nc.scalar.activation(kn_g[:, 0:HALF], kn_win[:].indirect(offsets[:, 0 : HALF // 16]), ACT.Copy)
+        kn_all = placed([P, N], F32, "kn_g", 32)
+        kn_g = [kn_all[:, 0:HALF], kn_all[:, HALF:N]]
 
         scale_g = sb.tile([P, N], U8, name="scale_g", align_bytes=64)
         nc.vector.tensor_copy(scale_g[:], scale_win[:].bitcast(U8).indirect(offsets[:]))
         for quad in range(4):
-            nc.scalar.dma_start(
+            queue = nc.sync if quad < 4 else nc.scalar
+            queue.dma_start(
                 k_planes[32 * quad : 32 * quad + 4, :],
                 scale_g[:].bitcast(I32)[96 + 8 * quad : 96 + 8 * quad + 8, :],
             )
+        load_last(1, 0)
+        nc.scalar.activation(kn_g[0], kn_win[:].indirect(offsets[:, 0:16]), ACT.Copy)
+        nc.scalar.activation(kn_g[1][:, 0:P], kn_win[:].indirect(offsets[:, 16:24]), ACT.Copy)
+        nc.vector.tensor_copy(kn_g[1][:, P:HALF], kn_win[:].indirect(offsets[:, 24:32]))
 
-        nc.vector.tensor_copy(kn_g[:, HALF:N], kn_win[:].indirect(offsets[:, HALF // 16 : N // 16]))
-        load_last(1, "kn_win")
-        kn_turned = ps.tile([P, 4, P], F32, name="kn_turned", tag="bank4")
-        for b in range(4):
-            nc.tensor.transpose(kn_turned[:, b, :], kn_g[:, P * b : P * (b + 1)], ident[:])
-        kn_col = shared.tile([P, 3 * SLOT // 4], F32, name="kn_col", offset=SLOT, align_bytes=64)
-        nc.scalar.copy(kn_col[:, 0:4], kn_turned[:, :, P - 1])
-        kn_spread = [ps.tile([P, HALF], F32, name="kn_spread%d" % h, tag="bank%d" % (6 + h)) for h in range(2)]
-        for b in range(4):
-            nc.tensor.transpose(
-                kn_spread[b // 2][:, P * (b % 2) : P * (b % 2 + 1)], kn_col[:, b : b + 1].to_broadcast([P, P]), ident[:]
-            )
-
-        word_g = sb.tile([P, N], U32, name="word_g", align_bytes=64)
+        kn_rows = sb.tile([P, N], F32, name="kn_rows", align_bytes=64)
         for h in range(2):
-            nc.vector.tensor_copy(
-                word_g[:, HALF * h : HALF * (h + 1)],
-                word_win[:].bitcast(U32).indirect(offsets[:, HALF // 16 * h : HALF // 16 * (h + 1)]),
-            )
-        k_codes = sb.tile([P, PASSES, 2 * N], U8, name="k_codes", align_bytes=64)
-        for h in range(2):
-            nc.vector.tensor_copy(
-                k_codes[:].bitcast(U16)[:, :, HALF * h : HALF * (h + 1)],
-                word_g[:, HALF * h : HALF * (h + 1)].bitcast(U16).rearrange("p (n o) -> p o n", o=PASSES),
-            )
+            kn_turned = ps.tile([P, 2, P], F32, name="kn_turned%d" % h, tag="bank%d" % (1 + h))
+            for b in range(2):
+                nc.tensor.transpose(kn_turned[:, b, :], kn_g[h][:, P * b : P * (b + 1)], ident[:])
+            kn_col = placed([P, 2], F32, "kn_col%d" % h, 30 + h / 16)
+            nc.scalar.copy(kn_col[:], kn_turned[:, :, P - 1])
+            kn_spread = ps.tile([P, HALF], F32, name="kn_spread%d" % h, tag="bank%d" % (6 + h))
+            for b in range(2):
+                nc.tensor.transpose(kn_spread[:, P * b : P * (b + 1)], kn_col[:, b : b + 1].to_broadcast([P, P]), ident[:])
+            nc.scalar.copy(kn_rows[:, HALF * h : HALF * (h + 1)], kn_spread[:])
+        qn_col = placed([P, QT], F32, "qn_col", 4)
+        nc.scalar.copy(qn_col[:], qn_turned[:, P - QT : P])
 
-        def interleave(o, j, slot, on_vector):
-            grouped = shared.tile([P, P, 4], BF16, name="grouped%d%d" % (o, j), offset=slot * SLOT, align_bytes=64)
-            for lo, hi, copy in ((0, P - on_vector, nc.scalar.copy), (P - on_vector, P, nc.vector.tensor_copy)):
-                if hi > lo:
-                    src = q_raw[(o, j)][:, :, lo:hi].rearrange("p t (c i) -> p c t i", i=4)
-                    copy(grouped[:, lo:hi, :].rearrange("p (c i) t -> p c t i", i=4), src)
-            return grouped
+        def copy_in(grouped, o, j, lo, hi, copy):
+            src = q_raw[(o, j)][:, :, lo:hi].rearrange("p t (c i) -> p c t i", i=4)
+            copy(grouped[:, lo:hi, :].rearrange("p (c i) t -> p c t i", i=4), src)
 
-        q_codes, q_planes = {}, {}
+        q_mx = {}
 
-        def quantise(o, j, grouped):
-            codes = sb.tile([P, P], U32, name="q_codes%d%d" % (o, j), align_bytes=64)
+        def quantise(o, j, grouped, slot):
+            codes = placed([P, P], U32, "q_codes%d%d" % (o, j), slot)
             plane = sb.tile([P, P], U8, name="q_plane%d%d" % (o, j), align_bytes=64)
             nc.vector.quantize_mx(
-                out=codes[:].bitcast(FP8X4), scales=plane[:], in_=grouped[:].rearrange("p m t -> p (m t)")
+                out=codes[:].bitcast(FP8X4), scales=plane[:], in_=grouped.rearrange("p m t -> p (m t)")
             )
-            q_codes[(o, j)], q_planes[(o, j)] = codes, plane
+            q_mx[(o, j)] = (codes, plane)
 
-        quantise(0, 0, interleave(0, 0, 0, 0))
-        kn_lo = sb.tile([P, HALF], F32, name="kn_lo", align_bytes=64)
-        nc.scalar.copy(kn_lo[:], kn_spread[0][:])
-        g10 = interleave(1, 0, 1, P // 2)
-        g01 = interleave(0, 1, 2, P)
-        kn_hi = shared.tile([P, HALF], F32, name="kn_hi", offset=3 * SLOT, align_bytes=64)
-        nc.scalar.copy(kn_hi[:], kn_spread[1][:])
-        quantise(1, 0, g10)
-        quantise(0, 1, g01)
-        quantise(1, 1, interleave(1, 1, 1, P // 2))
-        kn_rows = (kn_lo, kn_hi)
+        word_g = [placed([P, HALF], U32, "word_g%d" % h, 25 + h) for h in range(2)]
+        k_codes = [placed([P, PASSES, 2 * HALF], U8, "k_codes%d" % h, 27.25 + h) for h in range(2)]
 
-        def one_pass(o, g):
-            j, c, w = sums[g]
+        def part(h):
+            nc.vector.tensor_copy(
+                k_codes[h][:].bitcast(U16), word_g[h][:].bitcast(U16).rearrange("p (n o) -> p o n", o=PASSES)
+            )
+
+        for h in range(2):
+            nc.vector.tensor_copy(word_g[h][:], word_win[:].bitcast(U32).indirect(offsets[:, 16 * h : 16 * (h + 1)]))
+        g0 = placed([P, NQ, 4], BF16, "grouped0", 29.25)
+        g00, g01 = g0[:, 0:P, :], g0[:, P:NQ, :]
+        copy_in(g00, 0, 0, 0, 64, nc.scalar.copy)
+        copy_in(g00, 0, 0, 64, P, nc.vector.tensor_copy)
+        part(0)
+        quantise(0, 0, g00, 12)
+        part(1)
+        copy_in(g01, 0, 1, 0, 64, nc.scalar.copy)
+        g10 = placed([P, P, 4], BF16, "grouped10", 25)[:]
+        copy_in(g10, 1, 0, 0, 64, nc.scalar.copy)
+        copy_in(g10, 1, 0, 64, P, nc.vector.tensor_copy)
+        copy_in(g01, 0, 1, 64, P, nc.vector.tensor_copy)
+        quantise(1, 0, g10, 13)
+        quantise(0, 1, g01, 14)
+        g11 = placed([P, P, 4], BF16, "grouped11", 26)[:]
+        copy_in(g11, 1, 1, 0, 64, nc.scalar.copy)
+        copy_in(g11, 1, 1, 64, P, nc.vector.tensor_copy)
+        quantise(1, 1, g11, 15)
+
+        sums = ((0, 0, HALF), (0, HALF, HALF), (1, 0, P), (1, P, P), (1, HALF, P), (1, HALF + P, P))
+        acc = [ps.tile([P, w], F32, name="acc%d" % n, tag="bank%d" % n) for n, (j, c, w) in enumerate(sums)]
+
+        def one_pass(o, n):
+            j, c, w = sums[n]
+            h, lo = divmod(c, HALF)
             nc.tensor.matmul_mx(
-                out=acc[g][:],
-                lhsT=q_codes[(o, j)][:].bitcast(FP8X4),
-                lhsT_scale=q_planes[(o, j)][:],
-                rhs=k_codes[:, o, 2 * c : 2 * (c + w)].bitcast(FP4X4),
+                out=acc[n][:],
+                lhsT=q_mx[(o, j)][0][:].bitcast(FP8X4),
+                lhsT_scale=q_mx[(o, j)][1][:],
+                rhs=k_codes[h][:, o, 2 * lo : 2 * (lo + w)].bitcast(FP4X4),
                 rhs_scale=k_planes[:].bitcast(U8)[:, N * o + c : N * o + c + w],
                 start=(o == 0),
                 stop=(o == PASSES - 1),
             )
 
-        sums = [(j, P * b, P) for j in range(QT) for b in range(4)]
-        acc = [ps.tile([P, sums[g][2]], F32, name="acc%d" % g, tag="bank%d" % g) for g in range(len(sums))]
-        for groups in (range(0, 4), range(4, 6), range(6, 7), range(7, 8)):
-            for o in range(PASSES):
-                for g in groups:
-                    one_pass(o, g)
+        for o, group in ((0, range(0, 2)), (1, range(0, 2)), (0, range(2, 6)), (1, range(2, 6))):
+            for n in group:
+                one_pass(o, n)
 
-        res, part = {}, {}
-        for g, (j, c, w) in enumerate(sums):
+        res, summed = {}, {}
+        for n, (j, c, w) in enumerate(sums):
             h, lo = divmod(c, HALF)
             if lo == 0:
-                res[(j, h)] = sb.tile([P, HALF], F32, name="res%d_%d" % (j, h))
-                part[(j, h)] = sb.tile([P, HALF], F32, name="part%d_%d" % (j, h))
-            mine = part[(j, h)][:, lo : lo + w]
-            nc.vector.scalar_tensor_tensor(mine, acc[g][:], -2.0, kn_rows[h][:, lo : lo + w], ALU.mult, ALU.add)
-            if (j, h) != (1, 1):
+                res[(j, h)] = sb.tile([P, HALF], F32, name="res%d%d" % (j, h))
+                summed[(j, h)] = placed([P, HALF], F32, "summed%d%d" % (j, h), 2 * j + h)
+            mine = summed[(j, h)][:, lo : lo + w]
+            nc.vector.scalar_tensor_tensor(mine, acc[n][:], -2.0, kn_rows[:, c : c + w], ALU.mult, ALU.add)
+            if n < len(sums) - 1:
                 nc.scalar.activation(res[(j, h)][:, lo : lo + w], mine, ACT.Relu, bias=qn_col[:, j : j + 1])
-            elif lo + w == HALF:
-                nc.vector.tensor_scalar(res[(j, h)][:], part[(j, h)][:], qn_col[:, j : j + 1], 0.0, ALU.add, ALU.max)
+            elif n == len(sums) - 1:
+                last = slice(HALF - 1 * P, HALF)
+                nc.vector.tensor_scalar(res[(j, h)][:, last], summed[(j, h)][:, last], qn_col[:, j : j + 1], 0.0, ALU.add, ALU.max)
             if lo + w == HALF:
                 nc.sync.dma_start(out[0, P * j : P * (j + 1), HALF * h : HALF * (h + 1)], res[(j, h)][:])

@@ -83,7 +83,7 @@ def tile_attend_infodist_topk_kernel(tc, qT, k_words, k_scales, kn, qn, offs, ou
             channel_multiplier=1,
         )
 
-        qn_turned = ps.tile([P, P], F32, name="qn_turned", tag="bank0")
+        qn_turned = ps.tile([P, P], F32, name="qn_turned", tag="bank5")
         nc.tensor.transpose(qn_turned[:], qn_rows[:], ident[:])
 
         kn_all = placed([P, N], F32, "kn_g", 32)
@@ -102,19 +102,19 @@ def tile_attend_infodist_topk_kernel(tc, qT, k_words, k_scales, kn, qn, offs, ou
         nc.scalar.activation(kn_g[1][:, 0:P], kn_win[:].indirect(offsets[:, 16:24]), ACT.Copy)
         nc.vector.tensor_copy(kn_g[1][:, P:HALF], kn_win[:].indirect(offsets[:, 24:32]))
 
-        kn_rows = sb.tile([P, N], F32, name="kn_rows", align_bytes=64)
+        kn_spread = []
         for h in range(2):
             kn_turned = ps.tile([P, 2, P], F32, name="kn_turned%d" % h, tag="bank%d" % (1 + h))
             for b in range(2):
                 nc.tensor.transpose(kn_turned[:, b, :], kn_g[h][:, P * b : P * (b + 1)], ident[:])
             kn_col = placed([P, 2], F32, "kn_col%d" % h, 30 + h / 16)
             nc.scalar.copy(kn_col[:], kn_turned[:, :, P - 1])
-            kn_spread = ps.tile([P, HALF], F32, name="kn_spread%d" % h, tag="bank%d" % (6 + h))
+            kn_spread.append(ps.tile([P, HALF], F32, name="kn_spread%d" % h, tag="bank%d" % (7 - h)))
             for b in range(2):
-                nc.tensor.transpose(kn_spread[:, P * b : P * (b + 1)], kn_col[:, b : b + 1].to_broadcast([P, P]), ident[:])
-            nc.scalar.copy(kn_rows[:, HALF * h : HALF * (h + 1)], kn_spread[:])
-        qn_col = placed([P, QT], F32, "qn_col", 4)
-        nc.scalar.copy(qn_col[:], qn_turned[:, P - QT : P])
+                nc.tensor.transpose(kn_spread[h][:, P * b : P * (b + 1)], kn_col[:, b : b + 1].to_broadcast([P, P]), ident[:])
+            if h == 0:
+                kn_lo = sb.tile([P, HALF], F32, name="kn_lo", align_bytes=64)
+                nc.scalar.copy(kn_lo[:], kn_spread[0][:])
 
         def copy_in(grouped, o, j, lo, hi, copy):
             src = q_raw[(o, j)][:, :, lo:hi].rearrange("p t (c i) -> p c t i", i=4)
@@ -147,19 +147,22 @@ def tile_attend_infodist_topk_kernel(tc, qT, k_words, k_scales, kn, qn, offs, ou
         part(0)
         quantise(0, 0, g00, 12)
         part(1)
-        copy_in(g01, 0, 1, 0, 64, nc.scalar.copy)
+        copy_in(g01, 0, 1, 0, P, nc.scalar.copy)
         g10 = placed([P, P, 4], BF16, "grouped10", 25)[:]
         copy_in(g10, 1, 0, 0, 64, nc.scalar.copy)
         copy_in(g10, 1, 0, 64, P, nc.vector.tensor_copy)
-        copy_in(g01, 0, 1, 64, P, nc.vector.tensor_copy)
-        quantise(1, 0, g10, 13)
         quantise(0, 1, g01, 14)
-        g11 = placed([P, P, 4], BF16, "grouped11", 26)[:]
-        copy_in(g11, 1, 1, 0, 64, nc.scalar.copy)
-        copy_in(g11, 1, 1, 64, P, nc.vector.tensor_copy)
+        quantise(1, 0, g10, 13)
+        kn_hi = placed([P, HALF], F32, "kn_hi", 2)
+        nc.scalar.copy(kn_hi[:], kn_spread[1][:])
+        qn_col = placed([P, QT], F32, "qn_col", 3)
+        nc.scalar.copy(qn_col[:], qn_turned[:, P - QT : P])
+        kn_rows = (kn_lo, kn_hi)
+        g11 = placed([P, P, 4], BF16, "grouped11", 29.25)[:]
+        copy_in(g11, 1, 1, 0, P, nc.vector.tensor_copy)
         quantise(1, 1, g11, 15)
 
-        sums = ((0, 0, HALF), (0, HALF, HALF), (1, 0, P), (1, P, P), (1, HALF, P), (1, HALF + P, P))
+        sums = ((0, 0, P), (0, P, P), (0, HALF, HALF), (1, 0, P), (1, P, P), (1, HALF, P), (1, HALF + P, P))
         acc = [ps.tile([P, w], F32, name="acc%d" % n, tag="bank%d" % n) for n, (j, c, w) in enumerate(sums)]
 
         def one_pass(o, n):
@@ -175,7 +178,7 @@ def tile_attend_infodist_topk_kernel(tc, qT, k_words, k_scales, kn, qn, offs, ou
                 stop=(o == PASSES - 1),
             )
 
-        for o, group in ((0, range(0, 2)), (1, range(0, 2)), (0, range(2, 6)), (1, range(2, 6))):
+        for o, group in ((0, range(0, 5)), (1, range(0, 3)), (0, range(5, 7)), (1, range(3, 7))):
             for n in group:
                 one_pass(o, n)
 
@@ -184,9 +187,9 @@ def tile_attend_infodist_topk_kernel(tc, qT, k_words, k_scales, kn, qn, offs, ou
             h, lo = divmod(c, HALF)
             if lo == 0:
                 res[(j, h)] = sb.tile([P, HALF], F32, name="res%d%d" % (j, h))
-                summed[(j, h)] = placed([P, HALF], F32, "summed%d%d" % (j, h), 2 * j + h)
+                summed[(j, h)] = placed([P, HALF], F32, "summed%d%d" % (j, h), (0, 1, 34, 35)[2 * j + h])
             mine = summed[(j, h)][:, lo : lo + w]
-            nc.vector.scalar_tensor_tensor(mine, acc[n][:], -2.0, kn_rows[:, c : c + w], ALU.mult, ALU.add)
+            nc.vector.scalar_tensor_tensor(mine, acc[n][:], -2.0, kn_rows[h][:, lo : lo + w], ALU.mult, ALU.add)
             if n < len(sums) - 1:
                 nc.scalar.activation(res[(j, h)][:, lo : lo + w], mine, ACT.Relu, bias=qn_col[:, j : j + 1])
             elif n == len(sums) - 1:

@@ -83,17 +83,13 @@ def tile_attend_infodist_topk_kernel(tc, qT, k_words, k_scales, kn, qn, offs, ou
             channel_multiplier=1,
         )
 
-        qn_turned = ps.tile([P, P], F32, name="qn_turned", tag="bank5")
-        nc.tensor.transpose(qn_turned[:], qn_rows[:], ident[:])
-
         kn_all = placed([P, N], F32, "kn_g", 32)
         kn_g = [kn_all[:, 0:HALF], kn_all[:, HALF:N]]
 
         scale_g = sb.tile([P, N], U8, name="scale_g", align_bytes=64)
         nc.vector.tensor_copy(scale_g[:], scale_win[:].bitcast(U8).indirect(offsets[:]))
         for quad in range(4):
-            queue = nc.sync if quad < 4 else nc.scalar
-            queue.dma_start(
+            nc.sync.dma_start(
                 k_planes[32 * quad : 32 * quad + 4, :],
                 scale_g[:].bitcast(I32)[96 + 8 * quad : 96 + 8 * quad + 8, :],
             )
@@ -104,7 +100,7 @@ def tile_attend_infodist_topk_kernel(tc, qT, k_words, k_scales, kn, qn, offs, ou
 
         kn_spread = []
         for h in range(2):
-            kn_turned = ps.tile([P, 2, P], F32, name="kn_turned%d" % h, tag="bank%d" % (1 + h))
+            kn_turned = ps.tile([P, 2, P], F32, name="kn_turned%d" % h, tag="bank%d" % (1 + 4 * h))
             for b in range(2):
                 nc.tensor.transpose(kn_turned[:, b, :], kn_g[h][:, P * b : P * (b + 1)], ident[:])
             kn_col = placed([P, 2], F32, "kn_col%d" % h, 30 + h / 16)
@@ -115,6 +111,9 @@ def tile_attend_infodist_topk_kernel(tc, qT, k_words, k_scales, kn, qn, offs, ou
             if h == 0:
                 kn_lo = sb.tile([P, HALF], F32, name="kn_lo", align_bytes=64)
                 nc.scalar.copy(kn_lo[:], kn_spread[0][:])
+
+        qn_turned = ps.tile([P, P], F32, name="qn_turned", tag="bank5")
+        nc.tensor.transpose(qn_turned[:], qn_rows[:], ident[:])
 
         def copy_in(grouped, o, j, lo, hi, copy):
             src = q_raw[(o, j)][:, :, lo:hi].rearrange("p t (c i) -> p c t i", i=4)

@@ -37,6 +37,8 @@ def tile_attend_infodist_topk_kernel(tc, qT, k_words, k_scales, kn, qn, offs, ou
 
         zero_col = sb.tile([P, 1], F32, name="zero_col")
         nc.vector.memset(zero_col[:], 0.0)
+        kn_win = placed([P, T], F32, "kn_win", 4)
+        nc.scalar.dma_start(kn_win[127:128, :], kn[0:1, :])
         qn_rows = sb.tile([P, P], F32, name="qn_rows", align_bytes=64)
         nc.scalar.dma_start(qn_rows[P - QT : P, :], qn[0].rearrange("(j p) o -> j (p o)", p=P))
         nc.scalar.copy(qn_rows[0 : P - QT, :], zero_col[0 : P - QT, :].to_broadcast([P - QT, P]))
@@ -47,8 +49,6 @@ def tile_attend_infodist_topk_kernel(tc, qT, k_words, k_scales, kn, qn, offs, ou
         nc.sync.dma_start(scale_win[96:128, :], k_scales.bitcast(I32).rearrange("o f w -> f o w"))
         offsets = sb.tile([P, N // 16], U16, name="offsets")
         nc.sync.dma_start(offsets[:], offs)
-        kn_win = placed([P, T], F32, "kn_win", 4)
-        nc.sync.dma_start(kn_win[127:128, :], kn[0:1, :])
         word_win = placed([P, T], I32, "word_win", 12)
         nc.sync.dma_start(word_win[:], k_words[0].rearrange("p t b -> p (t b)").bitcast(I32))
 

@@ -161,8 +161,8 @@ def tile_attend_infodist_topk_kernel(tc, qT, k_words, k_scales, kn, qn, offs, ou
         copy_in(g11, 1, 1, 0, P, nc.vector.tensor_copy)
         quantise(1, 1, g11, 15)
 
-        sums = ((0, 0, P), (0, P, P), (0, HALF, HALF), (1, 0, P), (1, P, P), (1, HALF, P), (1, HALF + P, P))
-        acc = [ps.tile([P, w], F32, name="acc%d" % n, tag="bank%d" % n) for n, (j, c, w) in enumerate(sums)]
+        sums = ((0, 0, HALF), (0, HALF, HALF), (1, 0, HALF), (1, HALF, P), (1, HALF + P, P))
+        acc = [ps.tile([P, w], F32, name="acc%d" % n, tag="bank%d" % (0, 1, 2, 5, 6)[n]) for n, (j, c, w) in enumerate(sums)]
 
         def one_pass(o, n):
             j, c, w = sums[n]
@@ -177,7 +177,7 @@ def tile_attend_infodist_topk_kernel(tc, qT, k_words, k_scales, kn, qn, offs, ou
                 stop=(o == PASSES - 1),
             )
 
-        for o, group in ((0, range(0, 5)), (1, range(0, 3)), (0, range(5, 7)), (1, range(3, 7))):
+        for o, group in ((0, range(0, 3)), (1, range(0, 2)), (0, range(3, 5)), (1, range(2, 5))):
             for n in group:
                 one_pass(o, n)
 
@@ -187,12 +187,14 @@ def tile_attend_infodist_topk_kernel(tc, qT, k_words, k_scales, kn, qn, offs, ou
             if lo == 0:
                 res[(j, h)] = sb.tile([P, HALF], F32, name="res%d%d" % (j, h))
                 summed[(j, h)] = placed([P, HALF], F32, "summed%d%d" % (j, h), (0, 1, 34, 35)[2 * j + h])
-            mine = summed[(j, h)][:, lo : lo + w]
-            nc.vector.scalar_tensor_tensor(mine, acc[n][:], -2.0, kn_rows[h][:, lo : lo + w], ALU.mult, ALU.add)
-            if n < len(sums) - 1:
-                nc.scalar.activation(res[(j, h)][:, lo : lo + w], mine, ACT.Relu, bias=qn_col[:, j : j + 1])
-            elif n == len(sums) - 1:
-                last = slice(HALF - 1 * P, HALF)
-                nc.vector.tensor_scalar(res[(j, h)][:, last], summed[(j, h)][:, last], qn_col[:, j : j + 1], 0.0, ALU.add, ALU.max)
+            step = P
+            for a in range(0, w, step):
+                cols = slice(lo + a, lo + a + step)
+                mine = summed[(j, h)][:, cols]
+                nc.vector.scalar_tensor_tensor(mine, acc[n][:, a : a + step], -2.0, kn_rows[h][:, cols], ALU.mult, ALU.add)
+                if (j, c + a + step) != (QT - 1, N):
+                    nc.scalar.activation(res[(j, h)][:, cols], mine, ACT.Relu, bias=qn_col[:, j : j + 1])
+                else:
+                    nc.vector.tensor_scalar(res[(j, h)][:, cols], mine, qn_col[:, j : j + 1], 0.0, ALU.add, ALU.max)
             if lo + w == HALF:
                 nc.sync.dma_start(out[0, P * j : P * (j + 1), HALF * h : HALF * (h + 1)], res[(j, h)][:])

@@ -187,7 +187,7 @@ def tile_attend_infodist_topk_kernel(tc, qT, k_words, k_scales, kn, qn, offs, ou
             if lo == 0:
                 res[(j, h)] = sb.tile([P, HALF], F32, name="res%d%d" % (j, h))
                 summed[(j, h)] = placed([P, HALF], F32, "summed%d%d" % (j, h), (0, 1, 34, 35)[2 * j + h])
-            step = P
+            step = w if n == 1 else P
             for a in range(0, w, step):
                 cols = slice(lo + a, lo + a + step)
                 mine = summed[(j, h)][:, cols]

from contextlib import ExitStack

import concourse.mybir as mybir

N, T, D, NQ = 512, 2048, 1024, 256
FLOPS = 2 * NQ * N * D
BYTES = 4 * D * NQ + 128 * T * 4 + 32 * T + 4 * T + 4 * NQ + 128 * 32 * 2 + 4 * NQ * N

F32 = mybir.dt.float32
BF16 = mybir.dt.bfloat16
I32 = mybir.dt.int32
U32 = mybir.dt.uint32
U16 = mybir.dt.uint16
U8 = mybir.dt.uint8
FP8X4 = mybir.dt.float8_e4m3fn_x4
FP4X4 = mybir.dt.float4_e2m1fn_x4
ALU = mybir.AluOpType
ACT = mybir.ActivationFunctionType

P = 128
PASSES = 2
QT = 2
GROUPS = N // P
HALF = N // 2
SLOT = 1024


def tile_attend_infodist_topk_kernel(tc, qT, k_words, k_scales, kn, qn, offs, out):
    nc = tc.nc
    with ExitStack() as ctx:
        sb = ctx.enter_context(tc.tile_pool(name="sb", bufs=1))
        shared = ctx.enter_context(tc.tile_pool(name="shared", bufs=1))
        ps = ctx.enter_context(tc.psum_pool(name="ps", bufs=1))

        def placed(shape, dtype, name, slot):
            return shared.tile(shape, dtype, name=name, offset=int(slot * SLOT), align_bytes=64)

        zero_col = sb.tile([P, 1], F32, name="zero_col")
        nc.vector.memset(zero_col[:], 0.0)
        kn_win = placed([P, T], F32, "kn_win", 4)
        nc.scalar.dma_start(kn_win[127:128, :], kn[0:1, :])
        qn_rows = sb.tile([P, P], F32, name="qn_rows", align_bytes=64)
        nc.scalar.dma_start(qn_rows[P - QT : P, :], qn[0].rearrange("(j p) o -> j (p o)", p=P))
        nc.scalar.copy(qn_rows[0 : P - QT, :], zero_col[0 : P - QT, :].to_broadcast([P - QT, P]))
        zeros = sb.tile([P, P], F32, name="zeros", align_bytes=64)
        nc.gpsimd.memset(zeros[:], 0.0)

        scale_win = placed([P, T // 4], I32, "scale_win", 0)
        nc.sync.dma_start(scale_win[96:128, :], k_scales.bitcast(I32).rearrange("o f w -> f o w"))
        offsets = sb.tile([P, N // 16], U16, name="offsets")
        nc.sync.dma_start(offsets[:], offs)
        word_win = placed([P, T], I32, "word_win", 12)
        nc.sync.dma_start(word_win[:], k_words[0].rearrange("p t b -> p (t b)").bitcast(I32))

        def load_pass(o, slot):
            raw = placed([P, 4, NQ], F32, "q_raw%d" % o, slot)
            nc.sync.dma_start(raw[:], qT[0, 512 * o : 512 * (o + 1), :].rearrange("(p t) q -> p t q", t=4))
            return raw

        q_first = load_pass(0, 20)
        q_raw = {(0, j): q_first[:, :, P * j : P * (j + 1)] for j in range(QT)}

        def load_last(j, slot):
            raw = placed([P, 4, P], F32, "q_last%d" % j, slot)
            nc.sync.dma_start(raw[:], qT[0, 512:1024, P * j : P * (j + 1)].rearrange("(p t) q -> p t q", t=4))
            q_raw[(1, j)] = raw[:]

        load_last(0, 2)

        nc.vector.memset(scale_win[0:96, :], 0)
        k_planes = sb.tile([P, PASSES * N // 4], I32, name="k_planes", align_bytes=64)
        nc.vector.memset(k_planes[:], 0)
        nc.vector.memset(kn_win[0:127, 0 : 2048], 0.0)

        ident = placed([P, P], F32, "ident", 28)
        nc.gpsimd.affine_select(
            out=ident[:],
            in_=zeros[:],
            compare_op=ALU.not_equal,
            fill=1.0,
            base=0,
            pattern=[[-1, P]],
            channel_multiplier=1,
        )

        kn_all = placed([P, N], F32, "kn_g", 32)
        kn_g = [kn_all[:, 0:HALF], kn_all[:, HALF:N]]

        scale_g = sb.tile([P, N], U8, name="scale_g", align_bytes=64)
        nc.vector.tensor_copy(scale_g[:], scale_win[:].bitcast(U8).indirect(offsets[:]))
        for quad in range(4):
            nc.sync.dma_start(
                k_planes[32 * quad : 32 * quad + 4, :],
                scale_g[:].bitcast(I32)[96 + 8 * quad : 96 + 8 * quad + 8, :],
            )
        load_last(1, 0)
        nc.scalar.activation(kn_g[0], kn_win[:].indirect(offsets[:, 0:16]), ACT.Copy)
        nc.scalar.activation(kn_g[1][:, 0:P], kn_win[:].indirect(offsets[:, 16:24]), ACT.Copy)
        nc.vector.tensor_copy(kn_g[1][:, P:HALF], kn_win[:].indirect(offsets[:, 24:32]))

        kn_spread = []
        for h in range(2):
            kn_turned = ps.tile([P, 2, P], F32, name="kn_turned%d" % h, tag="bank%d" % (1 + 4 * h))
            for b in range(2):
                nc.tensor.transpose(kn_turned[:, b, :], kn_g[h][:, P * b : P * (b + 1)], ident[:])
            kn_col = placed([P, 2], F32, "kn_col%d" % h, 30 + h / 16)
            nc.scalar.copy(kn_col[:], kn_turned[:, :, P - 1])
            kn_spread.append(ps.tile([P, HALF], F32, name="kn_spread%d" % h, tag="bank%d" % (7 - h)))
            for b in range(2):
                nc.tensor.transpose(kn_spread[h][:, P * b : P * (b + 1)], kn_col[:, b : b + 1].to_broadcast([P, P]), ident[:])
            if h == 0:
                kn_lo = sb.tile([P, HALF], F32, name="kn_lo", align_bytes=64)
                nc.scalar.copy(kn_lo[:], kn_spread[0][:])

        qn_turned = ps.tile([P, P], F32, name="qn_turned", tag="bank5")
        nc.tensor.transpose(qn_turned[:], qn_rows[:], ident[:])

        def copy_in(grouped, o, j, lo, hi, copy):
            src = q_raw[(o, j)][:, :, lo:hi].rearrange("p t (c i) -> p c t i", i=4)
            copy(grouped[:, lo:hi, :].rearrange("p (c i) t -> p c t i", i=4), src)

        q_mx = {}

        def quantise(o, j, grouped, slot):
            codes = placed([P, P], U32, "q_codes%d%d" % (o, j), slot)
            plane = sb.tile([P, P], U8, name="q_plane%d%d" % (o, j), align_bytes=64)
            nc.vector.quantize_mx(
                out=codes[:].bitcast(FP8X4), scales=plane[:], in_=grouped.rearrange("p m t -> p (m t)")
            )
            q_mx[(o, j)] = (codes, plane)

        word_g = [placed([P, HALF], U32, "word_g%d" % h, 25 + h) for h in range(2)]
        k_codes = [placed([P, PASSES, 2 * HALF], U8, "k_codes%d" % h, 27.25 + h) for h in range(2)]

        def part(h):
            nc.vector.tensor_copy(
                k_codes[h][:].bitcast(U16), word_g[h][:].bitcast(U16).rearrange("p (n o) -> p o n", o=PASSES)
            )

        for h in range(2):
            nc.vector.tensor_copy(word_g[h][:], word_win[:].bitcast(U32).indirect(offsets[:, 16 * h : 16 * (h + 1)]))
        g0 = placed([P, NQ, 4], BF16, "grouped0", 29.25)
        g00, g01 = g0[:, 0:P, :], g0[:, P:NQ, :]
        copy_in(g00, 0, 0, 0, 64, nc.scalar.copy)
        copy_in(g00, 0, 0, 64, P, nc.vector.tensor_copy)
        part(0)
        quantise(0, 0, g00, 12)
        part(1)
        copy_in(g01, 0, 1, 0, P, nc.scalar.copy)
        g10 = placed([P, P, 4], BF16, "grouped10", 25)[:]
        copy_in(g10, 1, 0, 0, 64, nc.scalar.copy)
        copy_in(g10, 1, 0, 64, P, nc.vector.tensor_copy)
        quantise(0, 1, g01, 14)
        quantise(1, 0, g10, 13)
        kn_hi = placed([P, HALF], F32, "kn_hi", 2)
        nc.scalar.copy(kn_hi[:], kn_spread[1][:])
        qn_col = placed([P, QT], F32, "qn_col", 3)
        nc.scalar.copy(qn_col[:], qn_turned[:, P - QT : P])
        kn_rows = (kn_lo, kn_hi)
        g11 = placed([P, P, 4], BF16, "grouped11", 29.25)[:]
        copy_in(g11, 1, 1, 0, P, nc.vector.tensor_copy)
        quantise(1, 1, g11, 15)

        sums = ((0, 0, HALF), (0, HALF, HALF), (1, 0, HALF), (1, HALF, P), (1, HALF + P, P))
        acc = [ps.tile([P, w], F32, name="acc%d" % n, tag="bank%d" % (0, 1, 2, 5, 6)[n]) for n, (j, c, w) in enumerate(sums)]

        def one_pass(o, n):
            j, c, w = sums[n]
            h, lo = divmod(c, HALF)
            nc.tensor.matmul_mx(
                out=acc[n][:],
                lhsT=q_mx[(o, j)][0][:].bitcast(FP8X4),
                lhsT_scale=q_mx[(o, j)][1][:],
                rhs=k_codes[h][:, o, 2 * lo : 2 * (lo + w)].bitcast(FP4X4),
                rhs_scale=k_planes[:].bitcast(U8)[:, N * o + c : N * o + c + w],
                start=(o == 0),
                stop=(o == PASSES - 1),
            )

        for o, group in ((0, range(0, 3)), (1, range(0, 2)), (0, range(3, 5)), (1, range(2, 5))):
            for n in group:
                one_pass(o, n)

        res, summed = {}, {}
        for n, (j, c, w) in enumerate(sums):
            h, lo = divmod(c, HALF)
            if lo == 0:
                res[(j, h)] = sb.tile([P, HALF], F32, name="res%d%d" % (j, h))
                summed[(j, h)] = placed([P, HALF], F32, "summed%d%d" % (j, h), (0, 1, 34, 35)[2 * j + h])
            step = w if n == 1 else P
            for a in range(0, w, step):
                cols = slice(lo + a, lo + a + step)
                mine = summed[(j, h)][:, cols]
                nc.vector.scalar_tensor_tensor(mine, acc[n][:, a : a + step], -2.0, kn_rows[h][:, cols], ALU.mult, ALU.add)
                if (j, c + a + step) != (QT - 1, N):
                    nc.scalar.activation(res[(j, h)][:, cols], mine, ACT.Relu, bias=qn_col[:, j : j + 1])
                else:
                    nc.vector.tensor_scalar(res[(j, h)][:, cols], mine, qn_col[:, j : j + 1], 0.0, ALU.add, ALU.max)
            if lo + w == HALF:
                nc.sync.dma_start(out[0, P * j : P * (j + 1), HALF * h : HALF * (h + 1)], res[(j, h)][:])
